import numpy as np
import ml_dtypes


def mxq(x, axis, fmt="e4m3"):
    dtype, down = {"e4m3": (ml_dtypes.float8_e4m3fn, 7), "e5m2": (ml_dtypes.float8_e5m2, 14)}[fmt]
    v = np.moveaxis(np.asarray(x, np.float32).astype(ml_dtypes.bfloat16).astype(np.float64), axis, -1)
    blocks = v.reshape(v.shape[:-1] + (-1, 32))
    amax = np.abs(blocks).max(-1, keepdims=True)
    byte = np.maximum(np.where(amax > 0, np.frexp(amax)[1] - 1 + 127, 0) - down, 1)
    scale = np.exp2(byte - 127.0)
    codes = (blocks / scale).astype(np.float32).astype(dtype).astype(np.float64)
    return np.moveaxis((codes * scale).reshape(v.shape), -1, axis)


WIDE = False


def mx_kscale(k):
    if not WIDE:
        return np.ones(k)
    levels = np.array([10, -10, 5, -5, 0])
    if k % 512:
        return np.exp2(np.random.permutation(np.resize(levels, k // 32))).repeat(32)
    a = np.empty((k // 512, 16))
    for p in range(k // 512):
        a[p, :8] = np.random.permutation(np.resize(levels, 8))
        for g in range(8):
            far = levels[np.abs(levels - a[p, g]) >= 10]
            a[p, g + 8] = far[np.random.randint(len(far))]
    return np.exp2(a.ravel()).repeat(32)


def f64(x):
    return np.asarray(x).astype(np.float64)


def striped(idx):
    return np.tile(idx.reshape(-1, 16).T, (8, 1)).astype(np.uint16)


def unstriped(offs):
    return offs[:16].T.reshape(-1).astype(np.int64)


def pack_weight(w):
    k, n = w.shape
    w = f64(np.asarray(w, np.float32).astype(ml_dtypes.bfloat16)).reshape(k // 32, 32, n)
    amax = np.abs(w).max(1)
    byte = np.clip(np.where(amax > 0, np.frexp(amax)[1] - 1 + 127 - 7, 1), 1, 254)
    scaled = (w * np.exp2(127.0 - byte)[:, None, :]).reshape(k, n).astype(np.float32)
    words = np.ascontiguousarray(scaled.reshape(k // 512, 128, 4, n).transpose(0, 1, 3, 2)).astype(ml_dtypes.float8_e4m3fn).view(np.uint8)
    return words, np.ascontiguousarray(byte.astype(np.uint8).reshape(k // 512, 16, n))


def unpack_weight(words, scales):
    g, p, n, _ = words.shape
    vals = np.ascontiguousarray(words).view(ml_dtypes.float8_e4m3fn).astype(np.float64) * np.repeat(np.exp2(scales.astype(np.float64) - 127.0), 8, axis=1)[..., None]
    return vals.transpose(0, 1, 3, 2).reshape(g * 512, n)


def sigmoid(v):
    return 1.0 / (1.0 + np.exp(-np.maximum(v, -700.0)))


K, T, S, H, D, V, W, U, G = 512, 1024, 512, 512, 2, 256, 2048, 512, 1024


def setup_inputs():
    n = np.random.standard_normal
    s = mx_kscale(K)[:, None]
    u = mx_kscale(H)
    packed_xT = pack_weight(n((K, T)) * s)
    packed_eT = pack_weight(n((H, W)) / np.sqrt(H) / u[:, None])
    packed_dT = pack_weight(n((H, G)) / np.sqrt(H) / u[:, None])
    return {
        "x_words": packed_xT[0],
        "x_scales": packed_xT[1],
        "w1": (n((K, H)) / np.sqrt(K) / s * u).astype(np.float32),
        "e_words": packed_eT[0],
        "e_scales": packed_eT[1],
        "d_words": packed_dT[0],
        "d_scales": packed_dT[1],
        "offs": striped(np.random.permutation(T)[:S]),
        "user": striped(np.random.permutation(G)[:V]),
        "shown": striped(np.random.permutation(W)[:U]),
    }


def reference(x_words, x_scales, w1, e_words, e_scales, d_words, d_scales, offs, user, shown):
    xq = unpack_weight(x_words, x_scales)[:, unstriped(offs)]
    h = mxq(f64(w1), 0, "e4m3").T @ xq
    hq = mxq(h, 0, "e4m3")
    d_user = unpack_weight(d_words, d_scales)[:, unstriped(user)]
    y = hq.T @ d_user
    e_shown = unpack_weight(e_words, e_scales)[:, unstriped(shown)]
    z = hq.T @ e_shown
    near = z.reshape(len(z), -1, D).max(axis=2)
    return y * sigmoid(-2.0 * near)

@@ -1,0 +1,162 @@
+from contextlib import ExitStack
+
+import concourse.mybir as mybir
+
+K, T, S, H, D, V, W, U, G = 512, 1024, 512, 512, 2, 256, 2048, 512, 1024
+FLOPS = 2 * K * H * S + 2 * H * S * V + 2 * H * S * U
+
+F32 = mybir.dt.float32
+BF16 = mybir.dt.bfloat16
+I32 = mybir.dt.int32
+U32 = mybir.dt.uint32
+U16 = mybir.dt.uint16
+U8 = mybir.dt.uint8
+FP8X4 = mybir.dt.float8_e4m3fn_x4
+ALU = mybir.AluOpType
+ACT = mybir.ActivationFunctionType
+
+P = 128
+PACK = 4
+TILES = S // P
+HALF = H // 2
+
+
+def load_scale_rows(queue, tile, scales):
+    for q in range(4):
+        queue.dma_start(
+            out=tile[32 * q : 32 * q + 4, :].bitcast(I32),
+            in_=scales[0, 4 * q : 4 * q + 4, :].bitcast(I32),
+        )
+
+
+def load_words(nc, tile, words):
+    nc.sync.dma_start(out=tile[:], in_=words[0].rearrange("p n t -> p (n t)").bitcast(I32))
+
+
+def tile_picked_ymmr_soft_p_kernel(
+    tc, x_words, x_scales, w1, e_words, e_scales, d_words, d_scales, offs, user, shown, out
+):
+    nc = tc.nc
+    with ExitStack() as ctx:
+        lists = ctx.enter_context(tc.tile_pool(name="lists", bufs=1))
+        keep = ctx.enter_context(tc.tile_pool(name="keep", bufs=1))
+        psum = ctx.enter_context(tc.psum_pool(name="psum", bufs=8))
+
+        offs_t = lists.tile([P, S // 16], U16, name="offs_t")
+        shown_t = lists.tile([P, U // 16], U16, name="shown_t")
+        user_t = lists.tile([P, V // 16], U16, name="user_t")
+
+        xw = keep.tile([P, T], I32, name="xw", align_bytes=64)
+        ew = keep.tile([P, W], I32, name="ew", align_bytes=64)
+        dw = keep.tile([P, G], I32, name="dw", align_bytes=64)
+        xs = keep.tile([P, T], U8, name="xs", align_bytes=64)
+        es = keep.tile([P, W], U8, name="es", align_bytes=64)
+        ds = keep.tile([P, G], U8, name="ds", align_bytes=64)
+        warm = keep.tile([P, 8], F32, name="warm")
+        warm_out = keep.tile([P, 8], F32, name="warm_out")
+
+        nc.vector.memset(xs[:].bitcast(I32), 0)
+        nc.vector.memset(es[:].bitcast(I32), 0)
+        nc.gpsimd.memset(ds[:].bitcast(I32), 0)
+        nc.vector.memset(warm[:], 0.0)
+
+        nc.sync.dma_start(offs_t[:], offs)
+        nc.sync.dma_start(shown_t[:], shown)
+        nc.sync.dma_start(user_t[:], user)
+        load_scale_rows(nc.scalar, xs, x_scales)
+        nc.scalar.activation(warm_out[:], warm[:], ACT.Sigmoid, scale=-2.0)
+        load_words(nc, xw, x_words)
+        w_rows = w1.rearrange("(p j) c -> p j c", j=PACK)
+        w_raw = [keep.tile([P, PACK, HALF], F32, name="w_raw%d" % a) for a in range(2)]
+        for a in range(2):
+            nc.sync.dma_start(out=w_raw[a][:], in_=w_rows[:, :, a * HALF : (a + 1) * HALF])
+        load_scale_rows(nc.sync, es, e_scales)
+        load_scale_rows(nc.gpsimd, ds, d_scales)
+        load_words(nc, ew, e_words)
+        load_words(nc, dw, d_words)
+
+        xg_w = keep.tile([P, S], U32, name="xg_w", align_bytes=64)
+        xg_s = keep.tile([P, S], U8, name="xg_s", align_bytes=64)
+        eg_w = keep.tile([P, U], U32, name="eg_w", align_bytes=64)
+        eg_s = keep.tile([P, U], U8, name="eg_s", align_bytes=64)
+        dg_w = keep.tile([P, V], U32, name="dg_w", align_bytes=64)
+        dg_s = keep.tile([P, V], U8, name="dg_s", align_bytes=64)
+
+        nc.vector.tensor_copy(xg_s[:], xs[:].indirect(offs_t[:]))
+        nc.vector.tensor_copy(xg_w[:], xw[:].bitcast(U32).indirect(offs_t[:]))
+
+        w_bf = keep.tile([P, PACK, P, PACK], BF16, name="w_bf", align_bytes=64)
+        for a in range(2):
+            nc.scalar.copy(
+                w_bf[:, :, a * (P // 2) : (a + 1) * (P // 2), :].rearrange("p t m j -> p m t j"),
+                w_raw[a][:].rearrange("p j (m t) -> p m t j", t=PACK),
+            )
+        w_q = keep.tile([P, H], U32, name="w_q", align_bytes=64)
+        w_s = keep.tile([P, H], U8, name="w_s", align_bytes=64)
+        nc.vector.quantize_mx(
+            out=w_q[:].bitcast(FP8X4), scales=w_s[:], in_=w_bf[:].rearrange("p t m j -> p (t m j)")
+        )
+
+        nc.vector.tensor_copy(eg_s[:], es[:].indirect(shown_t[:]))
+
+        h_q, h_s = [], []
+        for i in range(TILES):
+            cols = slice(i * P, (i + 1) * P)
+            h_ps = psum.tile([P, PACK, P], F32, name="h_ps", tag="bank")
+            for t in range(PACK):
+                wc = slice(t * P, (t + 1) * P)
+                nc.tensor.matmul_mx(
+                    out=h_ps[:, t, :],
+                    lhsT=w_q[:, wc].bitcast(FP8X4),
+                    lhsT_scale=w_s[:, wc],
+                    rhs=xg_w[:, cols].bitcast(FP8X4),
+                    rhs_scale=xg_s[:, cols],
+                    start=True,
+                    stop=True,
+                )
+            h_bf = keep.tile([P, P, PACK], BF16, name="h_bf%d" % i, align_bytes=64)
+            nc.scalar.copy(h_bf[:], h_ps[:].rearrange("p t n -> p n t"))
+            codes = keep.tile([P, P], U32, name="h_q%d" % i, align_bytes=64)
+            planes = keep.tile([P, P], U8, name="h_s%d" % i, align_bytes=64)
+            nc.vector.quantize_mx(
+                out=codes[:].bitcast(FP8X4), scales=planes[:], in_=h_bf[:].rearrange("p n t -> p (n t)")
+            )
+            h_q.append(codes)
+            h_s.append(planes)
+
+        nc.vector.tensor_copy(eg_w[:], ew[:].bitcast(U32).indirect(shown_t[:]))
+        nc.vector.tensor_copy(dg_s[:], ds[:].indirect(user_t[:]))
+        nc.vector.tensor_copy(dg_w[:], dw[:].bitcast(U32).indirect(user_t[:]))
+
+        damp = []
+        for i in range(TILES):
+            z_ps = psum.tile([P, U], F32, name="z_ps", tag="bank")
+            nc.tensor.matmul_mx(
+                out=z_ps[:],
+                lhsT=h_q[i][:].bitcast(FP8X4),
+                lhsT_scale=h_s[i][:],
+                rhs=eg_w[:].bitcast(FP8X4),
+                rhs_scale=eg_s[:],
+                start=True,
+                stop=True,
+            )
+            sig = keep.tile([P, V, D], F32, name="sig%d" % i)
+            nc.scalar.activation(sig[:].rearrange("p v d -> p (v d)"), z_ps[:], ACT.Sigmoid, scale=-2.0)
+            low = keep.tile([P, V], F32, name="low%d" % i)
+            nc.vector.tensor_tensor(low[:], sig[:, :, 0], sig[:, :, 1], ALU.min)
+            damp.append(low)
+
+        for i in range(TILES):
+            y_ps = psum.tile([P, V], F32, name="y_ps", tag="bank")
+            nc.tensor.matmul_mx(
+                out=y_ps[:],
+                lhsT=h_q[i][:].bitcast(FP8X4),
+                lhsT_scale=h_s[i][:],
+                rhs=dg_w[:].bitcast(FP8X4),
+                rhs_scale=dg_s[:],
+                start=True,
+                stop=True,
+            )
+            res = keep.tile([P, V], F32, name="res%d" % i)
+            nc.vector.tensor_tensor(res[:], y_ps[:], damp[i][:], ALU.mult)
+            nc.sync.dma_start(out=out[i * P : (i + 1) * P, :], in_=res[:])

@@ -40,69 +40,83 @@ def tile_picked_ymmr_soft_p_kernel(
     with ExitStack() as ctx:
         lists = ctx.enter_context(tc.tile_pool(name="lists", bufs=1))
         keep = ctx.enter_context(tc.tile_pool(name="keep", bufs=1))
-        psum = ctx.enter_context(tc.psum_pool(name="psum", bufs=8))
+        reuse = ctx.enter_context(tc.tile_pool(name="reuse", bufs=1))
+        psum = ctx.enter_context(tc.psum_pool(name="psum", bufs=1))
 
         offs_t = lists.tile([P, S // 16], U16, name="offs_t")
         shown_t = lists.tile([P, U // 16], U16, name="shown_t")
         user_t = lists.tile([P, V // 16], U16, name="user_t")
 
         xw = keep.tile([P, T], I32, name="xw", align_bytes=64)
-        ew = keep.tile([P, W], I32, name="ew", align_bytes=64)
-        dw = keep.tile([P, G], I32, name="dw", align_bytes=64)
+        ew = keep.tile([P, W], I32, name="ew", tag="codes0", align_bytes=64)
+        dw = keep.tile([P, G], I32, name="dw", tag="codes1", align_bytes=64)
         xs = keep.tile([P, T], U8, name="xs", align_bytes=64)
         es = keep.tile([P, W], U8, name="es", align_bytes=64)
-        ds = keep.tile([P, G], U8, name="ds", align_bytes=64)
+        ds = keep.tile([P, G], U8, name="ds", tag="planes1", align_bytes=64)
         warm = keep.tile([P, 8], F32, name="warm")
         warm_out = keep.tile([P, 8], F32, name="warm_out")
 
-        nc.vector.memset(xs[:].bitcast(I32), 0)
-        nc.vector.memset(es[:].bitcast(I32), 0)
-        nc.gpsimd.memset(ds[:].bitcast(I32), 0)
-        nc.vector.memset(warm[:], 0.0)
+        nc.vector.memset(es[:, : W // 2].bitcast(I32), 0)
+        nc.gpsimd.memset(es[:, W // 2 :].bitcast(I32), 0)
+        nc.vector.memset(ds[:].bitcast(I32), 0)
+        nc.gpsimd.memset(warm[:], 0.0)
 
         nc.sync.dma_start(offs_t[:], offs)
-        nc.sync.dma_start(shown_t[:], shown)
-        nc.sync.dma_start(user_t[:], user)
-        load_scale_rows(nc.scalar, xs, x_scales)
+        for q in range(4):
+            (nc.sync if q < 2 else nc.scalar).dma_start(
+                out=xs[32 * q : 32 * q + 32, :].bitcast(I32),
+                in_=x_scales[0, 4 * q : 4 * q + 4, :].bitcast(I32).partition_broadcast(8),
+            )
         nc.scalar.activation(warm_out[:], warm[:], ACT.Sigmoid, scale=-2.0)
         load_words(nc, xw, x_words)
         w_rows = w1.rearrange("(p j) c -> p j c", j=PACK)
         w_raw = [keep.tile([P, PACK, HALF], F32, name="w_raw%d" % a) for a in range(2)]
-        for a in range(2):
-            nc.sync.dma_start(out=w_raw[a][:], in_=w_rows[:, :, a * HALF : (a + 1) * HALF])
+        nc.sync.dma_start(out=w_raw[0][:], in_=w_rows[:, :, :HALF])
+        nc.sync.dma_start(shown_t[:], shown)
         load_scale_rows(nc.sync, es, e_scales)
-        load_scale_rows(nc.gpsimd, ds, d_scales)
+        nc.sync.dma_start(out=w_raw[1][:], in_=w_rows[:, :, HALF:])
         load_words(nc, ew, e_words)
+        nc.sync.dma_start(user_t[:], user)
+        load_scale_rows(nc.sync, ds, d_scales)
         load_words(nc, dw, d_words)
 
         xg_w = keep.tile([P, S], U32, name="xg_w", align_bytes=64)
         xg_s = keep.tile([P, S], U8, name="xg_s", align_bytes=64)
-        eg_w = keep.tile([P, U], U32, name="eg_w", align_bytes=64)
         eg_s = keep.tile([P, U], U8, name="eg_s", align_bytes=64)
-        dg_w = keep.tile([P, V], U32, name="dg_w", align_bytes=64)
-        dg_s = keep.tile([P, V], U8, name="dg_s", align_bytes=64)
 
         nc.vector.tensor_copy(xg_s[:], xs[:].indirect(offs_t[:]))
         nc.vector.tensor_copy(xg_w[:], xw[:].bitcast(U32).indirect(offs_t[:]))
 
-        w_bf = keep.tile([P, PACK, P, PACK], BF16, name="w_bf", align_bytes=64)
-        for a in range(2):
-            nc.scalar.copy(
-                w_bf[:, :, a * (P // 2) : (a + 1) * (P // 2), :].rearrange("p t m j -> p m t j"),
-                w_raw[a][:].rearrange("p j (m t) -> p m t j", t=PACK),
-            )
-        w_q = keep.tile([P, H], U32, name="w_q", align_bytes=64)
-        w_s = keep.tile([P, H], U8, name="w_s", align_bytes=64)
-        nc.vector.quantize_mx(
-            out=w_q[:].bitcast(FP8X4), scales=w_s[:], in_=w_bf[:].rearrange("p t m j -> p (t m j)")
-        )
-
         nc.vector.tensor_copy(eg_s[:], es[:].indirect(shown_t[:]))
 
-        h_q, h_s = [], []
+        w_bf = reuse.tile([P, PACK, P, PACK], BF16, name="w_bf", align_bytes=64, offset=0)
+
+        def deal(copy, a, m0, m1):
+            copy(
+                w_bf[:, :, a * 64 + m0 : a * 64 + m1, :].rearrange("p t m j -> p m t j"),
+                w_raw[a][:, :, PACK * m0 : PACK * m1].rearrange("p j (m t) -> p m t j", t=PACK),
+            )
+
+        deal(nc.scalar.copy, 0, 0, 64)
+        deal(nc.scalar.copy, 1, 0, 24)
+        deal(nc.vector.tensor_copy, 1, 24, 64)
+        w_q = keep.tile([P, H], U32, name="w_q", align_bytes=64)
+        w_s = keep.tile([P, H], U8, name="w_s", align_bytes=64)
+        for a in range(2):
+            wc = slice(a * HALF, (a + 1) * HALF)
+            nc.vector.quantize_mx(
+                out=w_q[:, wc].bitcast(FP8X4),
+                scales=w_s[:, wc],
+                in_=w_bf[:, 2 * a : 2 * a + 2, :, :].rearrange("p t m j -> p (t m j)"),
+            )
+
+        eg_w = reuse.tile([P, U], U32, name="eg_w", align_bytes=64, offset=0)
+        nc.vector.tensor_copy(eg_w[:], ew[:].bitcast(U32).indirect(shown_t[:]))
+
+        h_q, h_s, h_bf = [], [], []
         for i in range(TILES):
             cols = slice(i * P, (i + 1) * P)
-            h_ps = psum.tile([P, PACK, P], F32, name="h_ps", tag="bank")
+            h_ps = psum.tile([P, PACK, P], F32, name="h_ps", tag="bank%d" % i)
             for t in range(PACK):
                 wc = slice(t * P, (t + 1) * P)
                 nc.tensor.matmul_mx(
@@ -114,49 +128,49 @@ def tile_picked_ymmr_soft_p_kernel(
                     start=True,
                     stop=True,
                 )
-            h_bf = keep.tile([P, P, PACK], BF16, name="h_bf%d" % i, align_bytes=64)
-            nc.scalar.copy(h_bf[:], h_ps[:].rearrange("p t n -> p n t"))
-            codes = keep.tile([P, P], U32, name="h_q%d" % i, align_bytes=64)
-            planes = keep.tile([P, P], U8, name="h_s%d" % i, align_bytes=64)
-            nc.vector.quantize_mx(
-                out=codes[:].bitcast(FP8X4), scales=planes[:], in_=h_bf[:].rearrange("p n t -> p (n t)")
-            )
-            h_q.append(codes)
-            h_s.append(planes)
+            stage = keep.tile([P, P, PACK], BF16, name="h_bf", tag="stage%d" % i, align_bytes=64)
+            nc.scalar.copy(stage[:], h_ps[:].rearrange("p t n -> p n t"))
+            h_bf.append(stage)
 
-        nc.vector.tensor_copy(eg_w[:], ew[:].bitcast(U32).indirect(shown_t[:]))
+        def quantise_pair(pair):
+            codes = keep.tile([P, 2, P], U32, name="h_codes", tag="codes%d" % pair, align_bytes=64)
+            planes = keep.tile([P, 2, P], U8, name="h_planes", tag="planes%d" % pair, align_bytes=64)
+            for r in range(2):
+                nc.vector.quantize_mx(
+                    out=codes[:, r, :].bitcast(FP8X4),
+                    scales=planes[:, r, :],
+                    in_=h_bf[2 * pair + r][:].rearrange("p n t -> p (n t)"),
+                )
+                h_q.append(codes[:, r, :])
+                h_s.append(planes[:, r, :])
+
+        def product(bank, i, words, scales):
+            nc.tensor.matmul_mx(
+                out=bank[:],
+                lhsT=h_q[i].bitcast(FP8X4),
+                lhsT_scale=h_s[i],
+                rhs=words[:].bitcast(FP8X4),
+                rhs_scale=scales[:],
+                start=True,
+                stop=True,
+            )
+
+        quantise_pair(0)
+        dg_s = keep.tile([P, V], U8, name="dg_s", tag="stage0", align_bytes=64)
+        dg_w = keep.tile([P, V], U32, name="dg_w", tag="stage1", align_bytes=64)
         nc.vector.tensor_copy(dg_s[:], ds[:].indirect(user_t[:]))
         nc.vector.tensor_copy(dg_w[:], dw[:].bitcast(U32).indirect(user_t[:]))
+        quantise_pair(1)
 
-        damp = []
         for i in range(TILES):
-            z_ps = psum.tile([P, U], F32, name="z_ps", tag="bank")
-            nc.tensor.matmul_mx(
-                out=z_ps[:],
-                lhsT=h_q[i][:].bitcast(FP8X4),
-                lhsT_scale=h_s[i][:],
-                rhs=eg_w[:].bitcast(FP8X4),
-                rhs_scale=eg_s[:],
-                start=True,
-                stop=True,
-            )
+            z_ps = psum.tile([P, U], F32, name="z_ps", tag="bank%d" % (4 + i))
+            product(z_ps, i, eg_w, eg_s)
+            y_ps = psum.tile([P, V], F32, name="y_ps", tag="bank%d" % i)
+            product(y_ps, i, dg_w, dg_s)
             sig = keep.tile([P, V, D], F32, name="sig%d" % i)
             nc.scalar.activation(sig[:].rearrange("p v d -> p (v d)"), z_ps[:], ACT.Sigmoid, scale=-2.0)
-            low = keep.tile([P, V], F32, name="low%d" % i)
+            low = keep.tile([P, V], F32, name="low", tag=("stage%d" % (3 - i) if i < 2 else "low%d" % i), align_bytes=64)
             nc.vector.tensor_tensor(low[:], sig[:, :, 0], sig[:, :, 1], ALU.min)
-            damp.append(low)
-
-        for i in range(TILES):
-            y_ps = psum.tile([P, V], F32, name="y_ps", tag="bank")
-            nc.tensor.matmul_mx(
-                out=y_ps[:],
-                lhsT=h_q[i][:].bitcast(FP8X4),
-                lhsT_scale=h_s[i][:],
-                rhs=dg_w[:].bitcast(FP8X4),
-                rhs_scale=dg_s[:],
-                start=True,
-                stop=True,
-            )
             res = keep.tile([P, V], F32, name="res%d" % i)
-            nc.vector.tensor_tensor(res[:], y_ps[:], damp[i][:], ALU.mult)
+            nc.vector.tensor_tensor(res[:], y_ps[:], low[:], ALU.mult)
             nc.sync.dma_start(out=out[i * P : (i + 1) * P, :], in_=res[:])

@@ -22,10 +22,10 @@ HALF = H // 2
 
 
 def load_scale_rows(queue, tile, scales):
-    for q in range(4):
+    for j in range(4):
         queue.dma_start(
-            out=tile[32 * q : 32 * q + 4, :].bitcast(I32),
-            in_=scales[0, 4 * q : 4 * q + 4, :].bitcast(I32),
+            out=tile[j:P:32, :].bitcast(I32),
+            in_=scales[0, j:16:4, :].bitcast(I32),
         )
 
 
@@ -48,11 +48,11 @@ def tile_picked_ymmr_soft_p_kernel(
         user_t = lists.tile([P, V // 16], U16, name="user_t")
 
         xw = keep.tile([P, T], I32, name="xw", align_bytes=64)
-        ew = keep.tile([P, W], I32, name="ew", tag="codes0", align_bytes=64)
-        dw = keep.tile([P, G], I32, name="dw", tag="codes1", align_bytes=64)
+        ew = reuse.tile([P, W], I32, name="ew", align_bytes=64, offset=8192)
+        dw = reuse.tile([P, G], I32, name="dw", align_bytes=64, offset=18432)
         xs = keep.tile([P, T], U8, name="xs", align_bytes=64)
-        es = keep.tile([P, W], U8, name="es", align_bytes=64)
-        ds = keep.tile([P, G], U8, name="ds", tag="planes1", align_bytes=64)
+        es = reuse.tile([P, W], U8, name="es", align_bytes=64, offset=4096)
+        ds = reuse.tile([P, G], U8, name="ds", align_bytes=64, offset=17408)
         warm = keep.tile([P, 8], F32, name="warm")
         warm_out = keep.tile([P, 8], F32, name="warm_out")
 
@@ -72,9 +72,9 @@ def tile_picked_ymmr_soft_p_kernel(
         w_rows = w1.rearrange("(p j) c -> p j c", j=PACK)
         w_raw = [keep.tile([P, PACK, HALF], F32, name="w_raw%d" % a) for a in range(2)]
         nc.sync.dma_start(out=w_raw[0][:], in_=w_rows[:, :, :HALF])
+        nc.sync.dma_start(out=w_raw[1][:], in_=w_rows[:, :, HALF:])
         nc.sync.dma_start(shown_t[:], shown)
         load_scale_rows(nc.sync, es, e_scales)
-        nc.sync.dma_start(out=w_raw[1][:], in_=w_rows[:, :, HALF:])
         load_words(nc, ew, e_words)
         nc.sync.dma_start(user_t[:], user)
         load_scale_rows(nc.sync, ds, d_scales)
@@ -82,12 +82,9 @@ def tile_picked_ymmr_soft_p_kernel(
 
         xg_w = keep.tile([P, S], U32, name="xg_w", align_bytes=64)
         xg_s = keep.tile([P, S], U8, name="xg_s", align_bytes=64)
-        eg_s = keep.tile([P, U], U8, name="eg_s", align_bytes=64)
 
         nc.vector.tensor_copy(xg_s[:], xs[:].indirect(offs_t[:]))
         nc.vector.tensor_copy(xg_w[:], xw[:].bitcast(U32).indirect(offs_t[:]))
-
-        nc.vector.tensor_copy(eg_s[:], es[:].indirect(shown_t[:]))
 
         w_bf = reuse.tile([P, PACK, P, PACK], BF16, name="w_bf", align_bytes=64, offset=0)
 
@@ -97,7 +94,8 @@ def tile_picked_ymmr_soft_p_kernel(
                 w_raw[a][:, :, PACK * m0 : PACK * m1].rearrange("p j (m t) -> p m t j", t=PACK),
             )
 
-        deal(nc.scalar.copy, 0, 0, 64)
+        deal(nc.scalar.copy, 0, 0, 32)
+        deal(nc.vector.tensor_copy, 0, 32, 64)
         deal(nc.scalar.copy, 1, 0, 24)
         deal(nc.vector.tensor_copy, 1, 24, 64)
         w_q = keep.tile([P, H], U32, name="w_q", align_bytes=64)
@@ -110,8 +108,9 @@ def tile_picked_ymmr_soft_p_kernel(
                 in_=w_bf[:, 2 * a : 2 * a + 2, :, :].rearrange("p t m j -> p (t m j)"),
             )
 
-        eg_w = reuse.tile([P, U], U32, name="eg_w", align_bytes=64, offset=0)
-        nc.vector.tensor_copy(eg_w[:], ew[:].bitcast(U32).indirect(shown_t[:]))
+        eg_s = keep.tile([P, U], U8, name="eg_s", align_bytes=64)
+        eg_w = keep.tile([P, U], U32, name="eg_w", align_bytes=64)
+        nc.vector.tensor_copy(eg_s[:], es[:].indirect(shown_t[:]))
 
         h_q, h_s, h_bf = [], [], []
         for i in range(TILES):
@@ -128,49 +127,55 @@ def tile_picked_ymmr_soft_p_kernel(
                     start=True,
                     stop=True,
                 )
-            stage = keep.tile([P, P, PACK], BF16, name="h_bf", tag="stage%d" % i, align_bytes=64)
+            stage = reuse.tile([P, P, PACK], BF16, name="h_bf%d" % i, align_bytes=64, offset=(6144, 22528, 23552, 16384)[i])
             nc.scalar.copy(stage[:], h_ps[:].rearrange("p t n -> p n t"))
             h_bf.append(stage)
 
-        def quantise_pair(pair):
-            codes = keep.tile([P, 2, P], U32, name="h_codes", tag="codes%d" % pair, align_bytes=64)
-            planes = keep.tile([P, 2, P], U8, name="h_planes", tag="planes%d" % pair, align_bytes=64)
-            for r in range(2):
-                nc.vector.quantize_mx(
-                    out=codes[:, r, :].bitcast(FP8X4),
-                    scales=planes[:, r, :],
-                    in_=h_bf[2 * pair + r][:].rearrange("p n t -> p (n t)"),
-                )
-                h_q.append(codes[:, r, :])
-                h_s.append(planes[:, r, :])
+        def quantise(i, at):
+            codes = reuse.tile([P, P], U32, name="h_codes%d" % i, align_bytes=64, offset=at)
+            planes = keep.tile([P, P], U8, name="h_planes%d" % i, align_bytes=64)
+            nc.vector.quantize_mx(
+                out=codes[:].bitcast(FP8X4),
+                scales=planes[:],
+                in_=h_bf[i][:].rearrange("p n t -> p (n t)"),
+            )
+            h_q.append(codes)
+            h_s.append(planes)
 
         def product(bank, i, words, scales):
             nc.tensor.matmul_mx(
                 out=bank[:],
-                lhsT=h_q[i].bitcast(FP8X4),
-                lhsT_scale=h_s[i],
+                lhsT=h_q[i][:].bitcast(FP8X4),
+                lhsT_scale=h_s[i][:],
                 rhs=words[:].bitcast(FP8X4),
                 rhs_scale=scales[:],
                 start=True,
                 stop=True,
             )
 
-        quantise_pair(0)
-        dg_s = keep.tile([P, V], U8, name="dg_s", tag="stage0", align_bytes=64)
-        dg_w = keep.tile([P, V], U32, name="dg_w", tag="stage1", align_bytes=64)
+        nc.vector.tensor_copy(eg_w[:], ew[:].bitcast(U32).indirect(shown_t[:]))
+        for i in range(TILES):
+            quantise(i, 8192 + 512 * i)
+        dg_s = keep.tile([P, V], U8, name="dg_s", align_bytes=64)
+        dg_w = keep.tile([P, V], U32, name="dg_w", align_bytes=64)
         nc.vector.tensor_copy(dg_s[:], ds[:].indirect(user_t[:]))
         nc.vector.tensor_copy(dg_w[:], dw[:].bitcast(U32).indirect(user_t[:]))
-        quantise_pair(1)
+
+        low, y_ps = [], []
+
+        def finish(i):
+            res = keep.tile([P, V], F32, name="res%d" % i)
+            nc.vector.tensor_tensor(res[:], y_ps[i][:], low[i][:], ALU.mult)
+            nc.sync.dma_start(out=out[i * P : (i + 1) * P, :], in_=res[:])
 
         for i in range(TILES):
             z_ps = psum.tile([P, U], F32, name="z_ps", tag="bank%d" % (4 + i))
             product(z_ps, i, eg_w, eg_s)
-            y_ps = psum.tile([P, V], F32, name="y_ps", tag="bank%d" % i)
-            product(y_ps, i, dg_w, dg_s)
-            sig = keep.tile([P, V, D], F32, name="sig%d" % i)
-            nc.scalar.activation(sig[:].rearrange("p v d -> p (v d)"), z_ps[:], ACT.Sigmoid, scale=-2.0)
-            low = keep.tile([P, V], F32, name="low", tag=("stage%d" % (3 - i) if i < 2 else "low%d" % i), align_bytes=64)
-            nc.vector.tensor_tensor(low[:], sig[:, :, 0], sig[:, :, 1], ALU.min)
-            res = keep.tile([P, V], F32, name="res%d" % i)
-            nc.vector.tensor_tensor(res[:], y_ps[:], low[:], ALU.mult)
-            nc.sync.dma_start(out=out[i * P : (i + 1) * P, :], in_=res[:])
+            sig = keep.tile([P, D, V], F32, name="sig%d" % i)
+            nc.scalar.activation(sig[:], z_ps[:].rearrange("p (v d) -> p d v", d=D), ACT.Sigmoid, scale=-2.0)
+            low.append(reuse.tile([P, V], F32, name="low%d" % i, align_bytes=64, offset=18432 + 1024 * i))
+            nc.vector.tensor_tensor(low[i][:], sig[:, 0, :], sig[:, 1, :], ALU.min)
+        for i in range(TILES):
+            y_ps.append(psum.tile([P, V], F32, name="y_ps", tag="bank%d" % i))
+            product(y_ps[i], i, dg_w, dg_s)
+            finish(i)

@@ -70,9 +70,9 @@ def tile_picked_ymmr_soft_p_kernel(
         nc.scalar.activation(warm_out[:], warm[:], ACT.Sigmoid, scale=-2.0)
         load_words(nc, xw, x_words)
         w_rows = w1.rearrange("(p j) c -> p j c", j=PACK)
-        w_raw = [keep.tile([P, PACK, HALF], F32, name="w_raw%d" % a) for a in range(2)]
-        nc.sync.dma_start(out=w_raw[0][:], in_=w_rows[:, :, :HALF])
-        nc.sync.dma_start(out=w_raw[1][:], in_=w_rows[:, :, HALF:])
+        w_raw = [keep.tile([P, 2, H], F32, name="w_raw%d" % a) for a in range(2)]
+        nc.sync.dma_start(out=w_raw[0][:], in_=w_rows[:, 0:2, :])
+        nc.sync.dma_start(out=w_raw[1][:], in_=w_rows[:, 2:4, :])
         nc.sync.dma_start(shown_t[:], shown)
         load_scale_rows(nc.sync, es, e_scales)
         load_words(nc, ew, e_words)
@@ -86,26 +86,23 @@ def tile_picked_ymmr_soft_p_kernel(
         nc.vector.tensor_copy(xg_s[:], xs[:].indirect(offs_t[:]))
         nc.vector.tensor_copy(xg_w[:], xw[:].bitcast(U32).indirect(offs_t[:]))
 
-        w_bf = reuse.tile([P, PACK, P, PACK], BF16, name="w_bf", align_bytes=64, offset=0)
-
-        def deal(copy, a, m0, m1):
-            copy(
-                w_bf[:, :, a * 64 + m0 : a * 64 + m1, :].rearrange("p t m j -> p m t j"),
-                w_raw[a][:, :, PACK * m0 : PACK * m1].rearrange("p j (m t) -> p m t j", t=PACK),
-            )
-
-        deal(nc.scalar.copy, 0, 0, 32)
-        deal(nc.vector.tensor_copy, 0, 32, 64)
-        deal(nc.scalar.copy, 1, 0, 24)
-        deal(nc.vector.tensor_copy, 1, 24, 64)
+        w_bf = [
+            reuse.tile([P, 2, P, PACK], BF16, name="w_bf%d" % u, align_bytes=64, offset=(0, 2048)[u]) for u in range(2)
+        ]
+        for a in range(2):
+            for u, copy in ((0, nc.scalar.copy), (1, nc.vector.tensor_copy)):
+                copy(
+                    w_bf[u][:, :, :, 2 * a : 2 * a + 2].rearrange("p t m j -> p m t j"),
+                    w_raw[a][:].rearrange("p j (m t) -> p m t j", t=PACK)[:, :, 2 * u : 2 * u + 2, :],
+                )
         w_q = keep.tile([P, H], U32, name="w_q", align_bytes=64)
         w_s = keep.tile([P, H], U8, name="w_s", align_bytes=64)
-        for a in range(2):
-            wc = slice(a * HALF, (a + 1) * HALF)
+        for u in (1, 0):
+            wc = slice(u * HALF, (u + 1) * HALF)
             nc.vector.quantize_mx(
                 out=w_q[:, wc].bitcast(FP8X4),
                 scales=w_s[:, wc],
-                in_=w_bf[:, 2 * a : 2 * a + 2, :, :].rearrange("p t m j -> p (t m j)"),
+                in_=w_bf[u][:].rearrange("p t m j -> p (t m j)"),
             )
 
         eg_s = keep.tile([P, U], U8, name="eg_s", align_bytes=64)
@@ -116,7 +113,7 @@ def tile_picked_ymmr_soft_p_kernel(
         for i in range(TILES):
             cols = slice(i * P, (i + 1) * P)
             h_ps = psum.tile([P, PACK, P], F32, name="h_ps", tag="bank%d" % i)
-            for t in range(PACK):
+            for t in (2, 3, 0, 1):
                 wc = slice(t * P, (t + 1) * P)
                 nc.tensor.matmul_mx(
                     out=h_ps[:, t, :],
@@ -161,21 +158,27 @@ def tile_picked_ymmr_soft_p_kernel(
         nc.vector.tensor_copy(dg_s[:], ds[:].indirect(user_t[:]))
         nc.vector.tensor_copy(dg_w[:], dw[:].bitcast(U32).indirect(user_t[:]))
 
-        low, y_ps = [], []
+        sig, y_ps, low = [], [], []
+        for i in range(TILES):
+            z_ps = psum.tile([P, U], F32, name="z_ps", tag="bank%d" % (4 + i))
+            product(z_ps, i, eg_w, eg_s)
+            sig.append(keep.tile([P, D, V], F32, name="sig%d" % i))
+            nc.scalar.activation(sig[i][:], z_ps[:].rearrange("p (v d) -> p d v", d=D), ACT.Sigmoid, scale=-2.0)
+        for i in range(TILES):
+            y_ps.append(psum.tile([P, V], F32, name="y_ps", tag="bank%d" % i))
+            product(y_ps[i], i, dg_w, dg_s)
+
+        def lesser(i):
+            low.append(reuse.tile([P, V], F32, name="low%d" % i, align_bytes=64, offset=18432 + 1024 * i))
+            nc.vector.tensor_tensor(low[i][:], sig[i][:, 0, :], sig[i][:, 1, :], ALU.min)
 
         def finish(i):
             res = keep.tile([P, V], F32, name="res%d" % i)
             nc.vector.tensor_tensor(res[:], y_ps[i][:], low[i][:], ALU.mult)
             nc.sync.dma_start(out=out[i * P : (i + 1) * P, :], in_=res[:])
 
-        for i in range(TILES):
-            z_ps = psum.tile([P, U], F32, name="z_ps", tag="bank%d" % (4 + i))
-            product(z_ps, i, eg_w, eg_s)
-            sig = keep.tile([P, D, V], F32, name="sig%d" % i)
-            nc.scalar.activation(sig[:], z_ps[:].rearrange("p (v d) -> p d v", d=D), ACT.Sigmoid, scale=-2.0)
-            low.append(reuse.tile([P, V], F32, name="low%d" % i, align_bytes=64, offset=18432 + 1024 * i))
-            nc.vector.tensor_tensor(low[i][:], sig[:, 0, :], sig[:, 1, :], ALU.min)
-        for i in range(TILES):
-            y_ps.append(psum.tile([P, V], F32, name="y_ps", tag="bank%d" % i))
-            product(y_ps[i], i, dg_w, dg_s)
-            finish(i)
+        for i in range(TILES + 2):
+            if i < TILES:
+                lesser(i)
+            if i >= 2:
+                finish(i - 2)

@@ -49,7 +49,7 @@ def tile_picked_ymmr_soft_p_kernel(
 
         xw = keep.tile([P, T], I32, name="xw", align_bytes=64)
         ew = reuse.tile([P, W], I32, name="ew", align_bytes=64, offset=8192)
-        dw = reuse.tile([P, G], I32, name="dw", align_bytes=64, offset=18432)
+        dw = keep.tile([P, G], I32, name="dw", align_bytes=64)
         xs = keep.tile([P, T], U8, name="xs", align_bytes=64)
         es = reuse.tile([P, W], U8, name="es", align_bytes=64, offset=4096)
         ds = reuse.tile([P, G], U8, name="ds", align_bytes=64, offset=17408)
@@ -61,12 +61,12 @@ def tile_picked_ymmr_soft_p_kernel(
         nc.vector.memset(ds[:].bitcast(I32), 0)
         nc.gpsimd.memset(warm[:], 0.0)
 
-        nc.sync.dma_start(offs_t[:], offs)
         for q in range(4):
             (nc.sync if q < 2 else nc.scalar).dma_start(
                 out=xs[32 * q : 32 * q + 32, :].bitcast(I32),
                 in_=x_scales[0, 4 * q : 4 * q + 4, :].bitcast(I32).partition_broadcast(8),
             )
+        nc.sync.dma_start(offs_t[:], offs)
         nc.scalar.activation(warm_out[:], warm[:], ACT.Sigmoid, scale=-2.0)
         load_words(nc, xw, x_words)
         w_rows = w1.rearrange("(p j) c -> p j c", j=PACK)
@@ -76,9 +76,9 @@ def tile_picked_ymmr_soft_p_kernel(
         nc.sync.dma_start(shown_t[:], shown)
         load_scale_rows(nc.sync, es, e_scales)
         load_words(nc, ew, e_words)
-        nc.sync.dma_start(user_t[:], user)
         load_scale_rows(nc.sync, ds, d_scales)
         load_words(nc, dw, d_words)
+        nc.sync.dma_start(user_t[:], user)
 
         xg_w = keep.tile([P, S], U32, name="xg_w", align_bytes=64)
         xg_s = keep.tile([P, S], U8, name="xg_s", align_bytes=64)
@@ -124,7 +124,7 @@ def tile_picked_ymmr_soft_p_kernel(
                     start=True,
                     stop=True,
                 )
-            stage = reuse.tile([P, P, PACK], BF16, name="h_bf%d" % i, align_bytes=64, offset=(6144, 22528, 23552, 16384)[i])
+            stage = keep.tile([P, P, PACK], BF16, name="h_bf%d" % i, align_bytes=64)
             nc.scalar.copy(stage[:], h_ps[:].rearrange("p t n -> p n t"))
             h_bf.append(stage)
 
@@ -158,7 +158,8 @@ def tile_picked_ymmr_soft_p_kernel(
         nc.vector.tensor_copy(dg_s[:], ds[:].indirect(user_t[:]))
         nc.vector.tensor_copy(dg_w[:], dw[:].bitcast(U32).indirect(user_t[:]))
 
-        sig, y_ps, low = [], [], []
+        sig, y_ps = [], []
+        low = reuse.tile([P, TILES, V], F32, name="low", align_bytes=64, offset=17408)
         for i in range(TILES):
             z_ps = psum.tile([P, U], F32, name="z_ps", tag="bank%d" % (4 + i))
             product(z_ps, i, eg_w, eg_s)
@@ -169,12 +170,11 @@ def tile_picked_ymmr_soft_p_kernel(
             product(y_ps[i], i, dg_w, dg_s)
 
         def lesser(i):
-            low.append(reuse.tile([P, V], F32, name="low%d" % i, align_bytes=64, offset=18432 + 1024 * i))
-            nc.vector.tensor_tensor(low[i][:], sig[i][:, 0, :], sig[i][:, 1, :], ALU.min)
+            nc.vector.tensor_tensor(low[:, i, :], sig[i][:, 0, :], sig[i][:, 1, :], ALU.min)
 
         def finish(i):
             res = keep.tile([P, V], F32, name="res%d" % i)
-            nc.vector.tensor_tensor(res[:], y_ps[i][:], low[i][:], ALU.mult)
+            nc.vector.tensor_tensor(res[:], y_ps[i][:], low[:, i, :], ALU.mult)
             nc.sync.dma_start(out=out[i * P : (i + 1) * P, :], in_=res[:])
 
         for i in range(TILES + 2):

@@ -21,14 +21,6 @@ TILES = S // P
 HALF = H // 2
 
 
-def load_scale_rows(queue, tile, scales):
-    for j in range(4):
-        queue.dma_start(
-            out=tile[j:P:32, :].bitcast(I32),
-            in_=scales[0, j:16:4, :].bitcast(I32),
-        )
-
-
 def load_words(nc, tile, words):
     nc.sync.dma_start(out=tile[:], in_=words[0].rearrange("p n t -> p (n t)").bitcast(I32))
 
@@ -48,56 +40,78 @@ def tile_picked_ymmr_soft_p_kernel(
         user_t = lists.tile([P, V // 16], U16, name="user_t")
 
         xw = keep.tile([P, T], I32, name="xw", align_bytes=64)
-        ew = reuse.tile([P, W], I32, name="ew", align_bytes=64, offset=8192)
-        dw = keep.tile([P, G], I32, name="dw", align_bytes=64)
-        xs = keep.tile([P, T], U8, name="xs", align_bytes=64)
-        es = reuse.tile([P, W], U8, name="es", align_bytes=64, offset=4096)
-        ds = reuse.tile([P, G], U8, name="ds", align_bytes=64, offset=17408)
+        ew = keep.tile([P, W], I32, name="ew", align_bytes=64)
+        xs = reuse.tile([P, T], U8, name="xs", align_bytes=64, offset=16384)
+        es = reuse.tile([P, W], U8, name="es", align_bytes=64, offset=0)
+        ds = keep.tile([P, G], U8, name="ds", align_bytes=64)
+        plane = keep.tile([P, U + V], U8, name="plane", align_bytes=64)
         warm = keep.tile([P, 8], F32, name="warm")
         warm_out = keep.tile([P, 8], F32, name="warm_out")
 
-        nc.vector.memset(es[:, : W // 2].bitcast(I32), 0)
-        nc.gpsimd.memset(es[:, W // 2 :].bitcast(I32), 0)
-        nc.vector.memset(ds[:].bitcast(I32), 0)
+        nc.gpsimd.memset(xs[:].bitcast(I32), 0)
         nc.gpsimd.memset(warm[:], 0.0)
+        nc.vector.memset(ds[:96, :].bitcast(I32), 0)
+        nc.vector.memset(es[:96, :].bitcast(I32), 0)
+        nc.vector.memset(plane[:].bitcast(I32), 0)
 
-        for q in range(4):
-            (nc.sync if q < 2 else nc.scalar).dma_start(
-                out=xs[32 * q : 32 * q + 32, :].bitcast(I32),
-                in_=x_scales[0, 4 * q : 4 * q + 4, :].bitcast(I32).partition_broadcast(8),
-            )
+        nc.sync.dma_start(user_t[:], user)
+        nc.scalar.dma_start(
+            out=ds[96:, :].bitcast(I32),
+            in_=d_scales[0].bitcast(I32).unsqueeze(1).broadcast_to([16, 2, G // 4]),
+        )
+        nc.sync.dma_start(shown_t[:], shown)
+        nc.scalar.dma_start(
+            out=es[96:, :].bitcast(I32),
+            in_=e_scales[0].bitcast(I32).unsqueeze(1).broadcast_to([16, 2, W // 4]),
+        )
         nc.sync.dma_start(offs_t[:], offs)
         nc.scalar.activation(warm_out[:], warm[:], ACT.Sigmoid, scale=-2.0)
-        load_words(nc, xw, x_words)
         w_rows = w1.rearrange("(p j) c -> p j c", j=PACK)
         w_raw = [keep.tile([P, 2, H], F32, name="w_raw%d" % a) for a in range(2)]
         nc.sync.dma_start(out=w_raw[0][:], in_=w_rows[:, 0:2, :])
         nc.sync.dma_start(out=w_raw[1][:], in_=w_rows[:, 2:4, :])
-        nc.sync.dma_start(shown_t[:], shown)
-        load_scale_rows(nc.sync, es, e_scales)
+        for j in range(4):
+            nc.sync.dma_start(out=xs[j:P:32, :].bitcast(I32), in_=x_scales[0, j:16:4, :].bitcast(I32))
+        x_flat = x_words[0].rearrange("p n t -> p (n t)").bitcast(I32)
+        for half in (slice(0, T // 2), slice(T // 2, T)):
+            nc.sync.dma_start(out=xw[:, half], in_=x_flat[:, half])
         load_words(nc, ew, e_words)
-        load_scale_rows(nc.sync, ds, d_scales)
+
+        picked = reuse.tile([P, U + V], U8, name="picked", align_bytes=64, offset=17408)
+        nc.vector.tensor_copy(picked[:, U:], ds[:].indirect(user_t[:]))
+        nc.vector.tensor_copy(picked[:, :U], es[:].indirect(shown_t[:]))
+        for j in range(4):
+            nc.sync.dma_start(out=plane[j:P:32, :].bitcast(I32), in_=picked[96 + 2 * j : P : 8, :].bitcast(I32))
+        dw = reuse.tile([P, G], I32, name="dw", align_bytes=64, offset=0)
         load_words(nc, dw, d_words)
-        nc.sync.dma_start(user_t[:], user)
-
-        xg_w = keep.tile([P, S], U32, name="xg_w", align_bytes=64)
-        xg_s = keep.tile([P, S], U8, name="xg_s", align_bytes=64)
-
-        nc.vector.tensor_copy(xg_s[:], xs[:].indirect(offs_t[:]))
-        nc.vector.tensor_copy(xg_w[:], xw[:].bitcast(U32).indirect(offs_t[:]))
 
         w_bf = [
-            reuse.tile([P, 2, P, PACK], BF16, name="w_bf%d" % u, align_bytes=64, offset=(0, 2048)[u]) for u in range(2)
+            reuse.tile([P, 2, P, PACK], BF16, name="w_bf%d" % u, align_bytes=64, offset=8192 + 2048 * u)
+            for u in range(2)
         ]
-        for a in range(2):
-            for u, copy in ((0, nc.scalar.copy), (1, nc.vector.tensor_copy)):
-                copy(
-                    w_bf[u][:, :, :, 2 * a : 2 * a + 2].rearrange("p t m j -> p m t j"),
-                    w_raw[a][:].rearrange("p j (m t) -> p m t j", t=PACK)[:, :, 2 * u : 2 * u + 2, :],
-                )
+
+        def cast(copy, a, u):
+            copy(
+                w_bf[u][:, :, :, 2 * a : 2 * a + 2].rearrange("p t m j -> p m t j"),
+                w_raw[a][:].rearrange("p j (m t) -> p m t j", t=PACK)[:, :, 2 * u : 2 * u + 2, :],
+            )
+
+        cast(nc.vector.tensor_copy, 0, 1)
+        cast(nc.scalar.copy, 0, 0)
+        cast(nc.scalar.copy, 1, 0)
+        cast(nc.scalar.copy, 1, 1)
+
+        xg_first = keep.tile([P, P], U32, name="xg_first", align_bytes=64)
+        xg_rest = reuse.tile([P, S - P], U32, name="xg_rest", align_bytes=64, offset=8192)
+
+        def xg_w(lo, hi):
+            return xg_first[:, lo:hi] if hi <= P else xg_rest[:, lo - P : hi - P]
+
+        xg_s = keep.tile([P, S], U8, name="xg_s", align_bytes=64)
         w_q = keep.tile([P, H], U32, name="w_q", align_bytes=64)
-        w_s = keep.tile([P, H], U8, name="w_s", align_bytes=64)
-        for u in (1, 0):
+        w_s = reuse.tile([P, H], U8, name="w_s", align_bytes=64, offset=16384)
+
+        def quantise_w(u):
             wc = slice(u * HALF, (u + 1) * HALF)
             nc.vector.quantize_mx(
                 out=w_q[:, wc].bitcast(FP8X4),
@@ -105,21 +119,27 @@ def tile_picked_ymmr_soft_p_kernel(
                 in_=w_bf[u][:].rearrange("p t m j -> p (t m j)"),
             )
 
-        eg_s = keep.tile([P, U], U8, name="eg_s", align_bytes=64)
-        eg_w = keep.tile([P, U], U32, name="eg_w", align_bytes=64)
-        nc.vector.tensor_copy(eg_s[:], es[:].indirect(shown_t[:]))
+        def pick_x(lo, hi):
+            nc.vector.tensor_copy(xg_w(lo, hi), xw[:].bitcast(U32).indirect(offs_t[:, lo // 16 : hi // 16]))
+
+        nc.vector.tensor_copy(xg_s[:], xs[:].indirect(offs_t[:]))
+        pick_x(0, P)
+        quantise_w(0)
+        quantise_w(1)
+        pick_x(P, 2 * P)
+        pick_x(2 * P, S)
 
         h_q, h_s, h_bf = [], [], []
         for i in range(TILES):
             cols = slice(i * P, (i + 1) * P)
             h_ps = psum.tile([P, PACK, P], F32, name="h_ps", tag="bank%d" % i)
-            for t in (2, 3, 0, 1):
+            for t in range(PACK):
                 wc = slice(t * P, (t + 1) * P)
                 nc.tensor.matmul_mx(
                     out=h_ps[:, t, :],
                     lhsT=w_q[:, wc].bitcast(FP8X4),
                     lhsT_scale=w_s[:, wc],
-                    rhs=xg_w[:, cols].bitcast(FP8X4),
+                    rhs=xg_w(i * P, (i + 1) * P).bitcast(FP8X4),
                     rhs_scale=xg_s[:, cols],
                     start=True,
                     stop=True,
@@ -128,9 +148,13 @@ def tile_picked_ymmr_soft_p_kernel(
             nc.scalar.copy(stage[:], h_ps[:].rearrange("p t n -> p n t"))
             h_bf.append(stage)
 
-        def quantise(i, at):
-            codes = reuse.tile([P, P], U32, name="h_codes%d" % i, align_bytes=64, offset=at)
-            planes = keep.tile([P, P], U8, name="h_planes%d" % i, align_bytes=64)
+        def quantise(i):
+            codes = reuse.tile(
+                [P, P], U32, name="h_codes%d" % i, align_bytes=64, offset=0 if i == 3 else 12288 + 512 * i
+            )
+            planes = reuse.tile(
+                [P, P], U8, name="h_planes%d" % i, align_bytes=64, offset=17408 + P * i
+            )
             nc.vector.quantize_mx(
                 out=codes[:].bitcast(FP8X4),
                 scales=planes[:],
@@ -145,29 +169,30 @@ def tile_picked_ymmr_soft_p_kernel(
                 lhsT=h_q[i][:].bitcast(FP8X4),
                 lhsT_scale=h_s[i][:],
                 rhs=words[:].bitcast(FP8X4),
-                rhs_scale=scales[:],
+                rhs_scale=scales,
                 start=True,
                 stop=True,
             )
 
-        nc.vector.tensor_copy(eg_w[:], ew[:].bitcast(U32).indirect(shown_t[:]))
-        for i in range(TILES):
-            quantise(i, 8192 + 512 * i)
-        dg_s = keep.tile([P, V], U8, name="dg_s", align_bytes=64)
+        eg_w = keep.tile([P, U], U32, name="eg_w", align_bytes=64)
         dg_w = keep.tile([P, V], U32, name="dg_w", align_bytes=64)
-        nc.vector.tensor_copy(dg_s[:], ds[:].indirect(user_t[:]))
+        quantise(0)
+        nc.vector.tensor_copy(eg_w[:], ew[:].bitcast(U32).indirect(shown_t[:]))
+        quantise(1)
+        quantise(2)
         nc.vector.tensor_copy(dg_w[:], dw[:].bitcast(U32).indirect(user_t[:]))
+        quantise(3)
 
         sig, y_ps = [], []
-        low = reuse.tile([P, TILES, V], F32, name="low", align_bytes=64, offset=17408)
+        low = reuse.tile([P, TILES, V], F32, name="low", align_bytes=64, offset=512)
         for i in range(TILES):
             z_ps = psum.tile([P, U], F32, name="z_ps", tag="bank%d" % (4 + i))
-            product(z_ps, i, eg_w, eg_s)
+            product(z_ps, i, eg_w, plane[:, :U])
             sig.append(keep.tile([P, D, V], F32, name="sig%d" % i))
             nc.scalar.activation(sig[i][:], z_ps[:].rearrange("p (v d) -> p d v", d=D), ACT.Sigmoid, scale=-2.0)
         for i in range(TILES):
             y_ps.append(psum.tile([P, V], F32, name="y_ps", tag="bank%d" % i))
-            product(y_ps[i], i, dg_w, dg_s)
+            product(y_ps[i], i, dg_w, plane[:, U:])
 
         def lesser(i):
             nc.vector.tensor_tensor(low[:, i, :], sig[i][:, 0, :], sig[i][:, 1, :], ALU.min)
@@ -177,8 +202,8 @@ def tile_picked_ymmr_soft_p_kernel(
             nc.vector.tensor_tensor(res[:], y_ps[i][:], low[:, i, :], ALU.mult)
             nc.sync.dma_start(out=out[i * P : (i + 1) * P, :], in_=res[:])
 
-        for i in range(TILES + 2):
+        for i in range(TILES + 1):
             if i < TILES:
                 lesser(i)
-            if i >= 2:
-                finish(i - 2)
+            if i >= 1:
+                finish(i - 1)

@@ -64,17 +64,15 @@ def tile_picked_ymmr_soft_p_kernel(
             out=es[96:, :].bitcast(I32),
             in_=e_scales[0].bitcast(I32).unsqueeze(1).broadcast_to([16, 2, W // 4]),
         )
-        nc.sync.dma_start(offs_t[:], offs)
         nc.scalar.activation(warm_out[:], warm[:], ACT.Sigmoid, scale=-2.0)
         w_rows = w1.rearrange("(p j) c -> p j c", j=PACK)
         w_raw = [keep.tile([P, 2, H], F32, name="w_raw%d" % a) for a in range(2)]
         nc.sync.dma_start(out=w_raw[0][:], in_=w_rows[:, 0:2, :])
+        nc.sync.dma_start(offs_t[:], offs)
         nc.sync.dma_start(out=w_raw[1][:], in_=w_rows[:, 2:4, :])
         for j in range(4):
             nc.sync.dma_start(out=xs[j:P:32, :].bitcast(I32), in_=x_scales[0, j:16:4, :].bitcast(I32))
-        x_flat = x_words[0].rearrange("p n t -> p (n t)").bitcast(I32)
-        for half in (slice(0, T // 2), slice(T // 2, T)):
-            nc.sync.dma_start(out=xw[:, half], in_=x_flat[:, half])
+        load_words(nc, xw, x_words)
         load_words(nc, ew, e_words)
 
         picked = reuse.tile([P, U + V], U8, name="picked", align_bytes=64, offset=17408)
@@ -183,27 +181,34 @@ def tile_picked_ymmr_soft_p_kernel(
         nc.vector.tensor_copy(dg_w[:], dw[:].bitcast(U32).indirect(user_t[:]))
         quantise(3)
 
+        def pieces(i):
+            return [(0, V // 2), (V // 2, V)] if i == TILES - 1 else [(0, V)]
+
         sig, y_ps = [], []
         low = reuse.tile([P, TILES, V], F32, name="low", align_bytes=64, offset=512)
         for i in range(TILES):
             z_ps = psum.tile([P, U], F32, name="z_ps", tag="bank%d" % (4 + i))
             product(z_ps, i, eg_w, plane[:, :U])
             sig.append(keep.tile([P, D, V], F32, name="sig%d" % i))
-            nc.scalar.activation(sig[i][:], z_ps[:].rearrange("p (v d) -> p d v", d=D), ACT.Sigmoid, scale=-2.0)
+            pairs = z_ps[:].rearrange("p (v d) -> p d v", d=D)
+            for lo, hi in pieces(i):
+                nc.scalar.activation(sig[i][:, :, lo:hi], pairs[:, :, lo:hi], ACT.Sigmoid, scale=-2.0)
         for i in range(TILES):
             y_ps.append(psum.tile([P, V], F32, name="y_ps", tag="bank%d" % i))
             product(y_ps[i], i, dg_w, plane[:, U:])
 
-        def lesser(i):
-            nc.vector.tensor_tensor(low[:, i, :], sig[i][:, 0, :], sig[i][:, 1, :], ALU.min)
+        res = [keep.tile([P, V], F32, name="res%d" % i) for i in range(TILES)]
 
-        def finish(i):
-            res = keep.tile([P, V], F32, name="res%d" % i)
-            nc.vector.tensor_tensor(res[:], y_ps[i][:], low[:, i, :], ALU.mult)
-            nc.sync.dma_start(out=out[i * P : (i + 1) * P, :], in_=res[:])
+        def lesser(i, lo, hi):
+            nc.vector.tensor_tensor(low[:, i, lo:hi], sig[i][:, 0, lo:hi], sig[i][:, 1, lo:hi], ALU.min)
 
-        for i in range(TILES + 1):
-            if i < TILES:
-                lesser(i)
-            if i >= 1:
-                finish(i - 1)
+        def finish(i, lo, hi):
+            nc.vector.tensor_tensor(res[i][:, lo:hi], y_ps[i][:, lo:hi], low[:, i, lo:hi], ALU.mult)
+            nc.sync.dma_start(out=out[i * P : (i + 1) * P, lo:hi], in_=res[i][:, lo:hi])
+
+        steps = [(i, lo, hi) for i in range(TILES) for lo, hi in pieces(i)]
+        for n in range(len(steps) + 1):
+            if n < len(steps):
+                lesser(*steps[n])
+            if n >= 1:
+                finish(*steps[n - 1])

@@ -39,12 +39,12 @@ def tile_picked_ymmr_soft_p_kernel(
         shown_t = lists.tile([P, U // 16], U16, name="shown_t")
         user_t = lists.tile([P, V // 16], U16, name="user_t")
 
-        xw = keep.tile([P, T], I32, name="xw", align_bytes=64)
-        ew = keep.tile([P, W], I32, name="ew", align_bytes=64)
-        xs = reuse.tile([P, T], U8, name="xs", align_bytes=64, offset=16384)
-        es = reuse.tile([P, W], U8, name="es", align_bytes=64, offset=0)
-        ds = keep.tile([P, G], U8, name="ds", align_bytes=64)
-        plane = keep.tile([P, U + V], U8, name="plane", align_bytes=64)
+        xw = keep.tile([P, T], I32, name="xw", align_bytes=256)
+        ew = keep.tile([P, W], I32, name="ew", align_bytes=256)
+        xs = reuse.tile([P, T], U8, name="xs", align_bytes=256, offset=16384)
+        es = reuse.tile([P, W], U8, name="es", align_bytes=256, offset=0)
+        ds = keep.tile([P, G], U8, name="ds", align_bytes=256)
+        plane = keep.tile([P, U + V], U8, name="plane", align_bytes=256)
         warm = keep.tile([P, 8], F32, name="warm")
         warm_out = keep.tile([P, 8], F32, name="warm_out")
 
@@ -66,7 +66,7 @@ def tile_picked_ymmr_soft_p_kernel(
         )
         nc.scalar.activation(warm_out[:], warm[:], ACT.Sigmoid, scale=-2.0)
         w_rows = w1.rearrange("(p j) c -> p j c", j=PACK)
-        w_raw = [keep.tile([P, 2, H], F32, name="w_raw%d" % a) for a in range(2)]
+        w_raw = [keep.tile([P, 2, H], F32, name="w_raw%d" % a, align_bytes=256) for a in range(2)]
         nc.sync.dma_start(out=w_raw[0][:], in_=w_rows[:, 0:2, :])
         nc.sync.dma_start(offs_t[:], offs)
         nc.sync.dma_start(out=w_raw[1][:], in_=w_rows[:, 2:4, :])
@@ -75,12 +75,12 @@ def tile_picked_ymmr_soft_p_kernel(
         load_words(nc, xw, x_words)
         load_words(nc, ew, e_words)
 
-        picked = reuse.tile([P, U + V], U8, name="picked", align_bytes=64, offset=17408)
+        picked = reuse.tile([P, U + V], U8, name="picked", align_bytes=256, offset=17408)
         nc.vector.tensor_copy(picked[:, U:], ds[:].indirect(user_t[:]))
         nc.vector.tensor_copy(picked[:, :U], es[:].indirect(shown_t[:]))
         for j in range(4):
             nc.sync.dma_start(out=plane[j:P:32, :].bitcast(I32), in_=picked[96 + 2 * j : P : 8, :].bitcast(I32))
-        dw = reuse.tile([P, G], I32, name="dw", align_bytes=64, offset=0)
+        dw = reuse.tile([P, G], I32, name="dw", align_bytes=256, offset=0)
         load_words(nc, dw, d_words)
 
         w_bf = [
@@ -197,7 +197,7 @@ def tile_picked_ymmr_soft_p_kernel(
             y_ps.append(psum.tile([P, V], F32, name="y_ps", tag="bank%d" % i))
             product(y_ps[i], i, dg_w, plane[:, U:])
 
-        res = [keep.tile([P, V], F32, name="res%d" % i) for i in range(TILES)]
+        res = [keep.tile([P, V], F32, name="res%d" % i, align_bytes=256) for i in range(TILES)]
 
         def lesser(i, lo, hi):
             nc.vector.tensor_tensor(low[:, i, lo:hi], sig[i][:, 0, lo:hi], sig[i][:, 1, lo:hi], ALU.min)

@@ -148,7 +148,7 @@ def tile_picked_ymmr_soft_p_kernel(
 
         def quantise(i):
             codes = reuse.tile(
-                [P, P], U32, name="h_codes%d" % i, align_bytes=64, offset=0 if i == 3 else 12288 + 512 * i
+                [P, P], U32, name="h_codes%d" % i, align_bytes=64, offset=512 * (i - 2) if i >= 2 else 12288 + 512 * i
             )
             planes = reuse.tile(
                 [P, P], U8, name="h_planes%d" % i, align_bytes=64, offset=17408 + P * i
@@ -177,25 +177,33 @@ def tile_picked_ymmr_soft_p_kernel(
         quantise(0)
         nc.vector.tensor_copy(eg_w[:], ew[:].bitcast(U32).indirect(shown_t[:]))
         quantise(1)
-        quantise(2)
         nc.vector.tensor_copy(dg_w[:], dw[:].bitcast(U32).indirect(user_t[:]))
+        quantise(2)
         quantise(3)
 
         def pieces(i):
-            return [(0, V // 2), (V // 2, V)] if i == TILES - 1 else [(0, V)]
+            return [(0, V // 2), (V // 2, V)]
 
         sig, y_ps = [], []
-        low = reuse.tile([P, TILES, V], F32, name="low", align_bytes=64, offset=512)
-        for i in range(TILES):
+        low = reuse.tile([P, TILES, V], F32, name="low", align_bytes=64, offset=1024)
+
+        def seen(i):
             z_ps = psum.tile([P, U], F32, name="z_ps", tag="bank%d" % (4 + i))
             product(z_ps, i, eg_w, plane[:, :U])
             sig.append(keep.tile([P, D, V], F32, name="sig%d" % i))
             pairs = z_ps[:].rearrange("p (v d) -> p d v", d=D)
             for lo, hi in pieces(i):
                 nc.scalar.activation(sig[i][:, :, lo:hi], pairs[:, :, lo:hi], ACT.Sigmoid, scale=-2.0)
-        for i in range(TILES):
+
+        def score(i):
             y_ps.append(psum.tile([P, V], F32, name="y_ps", tag="bank%d" % i))
             product(y_ps[i], i, dg_w, plane[:, U:])
+
+        for pair in ((0, 1), (2, 3)):
+            for i in pair:
+                seen(i)
+            for i in pair:
+                score(i)
 
         res = [keep.tile([P, V], F32, name="res%d" % i, align_bytes=256) for i in range(TILES)]
 
@@ -204,7 +212,10 @@ def tile_picked_ymmr_soft_p_kernel(
 
         def finish(i, lo, hi):
             nc.vector.tensor_tensor(res[i][:, lo:hi], y_ps[i][:, lo:hi], low[:, i, lo:hi], ALU.mult)
-            nc.sync.dma_start(out=out[i * P : (i + 1) * P, lo:hi], in_=res[i][:, lo:hi])
+            if i == TILES - 1:
+                nc.sync.dma_start(out=out[i * P : (i + 1) * P, lo:hi], in_=res[i][:, lo:hi])
+            elif hi == V:
+                nc.sync.dma_start(out=out[i * P : (i + 1) * P, :], in_=res[i][:])
 
         steps = [(i, lo, hi) for i in range(TILES) for lo, hi in pieces(i)]
         for n in range(len(steps) + 1):

@@ -41,7 +41,7 @@ def tile_picked_ymmr_soft_p_kernel(
 
         xw = keep.tile([P, T], I32, name="xw", align_bytes=256)
         ew = keep.tile([P, W], I32, name="ew", align_bytes=256)
-        xs = reuse.tile([P, T], U8, name="xs", align_bytes=256, offset=16384)
+        xs = keep.tile([P, T], U8, name="xs", align_bytes=256)
         es = reuse.tile([P, W], U8, name="es", align_bytes=256, offset=0)
         ds = keep.tile([P, G], U8, name="ds", align_bytes=256)
         plane = keep.tile([P, U + V], U8, name="plane", align_bytes=256)
@@ -67,11 +67,15 @@ def tile_picked_ymmr_soft_p_kernel(
         nc.scalar.activation(warm_out[:], warm[:], ACT.Sigmoid, scale=-2.0)
         w_rows = w1.rearrange("(p j) c -> p j c", j=PACK)
         w_raw = [keep.tile([P, 2, H], F32, name="w_raw%d" % a, align_bytes=256) for a in range(2)]
-        nc.sync.dma_start(out=w_raw[0][:], in_=w_rows[:, 0:2, :])
+        second = w_rows[:, 2:4, :].rearrange("p j c -> p (j c)")
+        second_raw = w_raw[1][:].rearrange("p j c -> p (j c)")
+        body = 2 * H - 16
         nc.sync.dma_start(offs_t[:], offs)
-        nc.sync.dma_start(out=w_raw[1][:], in_=w_rows[:, 2:4, :])
+        nc.sync.dma_start(out=w_raw[0][:], in_=w_rows[:, 0:2, :])
+        nc.sync.dma_start(out=second_raw[:, :body], in_=second[:, :body])
         for j in range(4):
             nc.sync.dma_start(out=xs[j:P:32, :].bitcast(I32), in_=x_scales[0, j:16:4, :].bitcast(I32))
+        nc.sync.dma_start(out=second_raw[:, body:], in_=second[:, body:])
         load_words(nc, xw, x_words)
         load_words(nc, ew, e_words)
 
@@ -88,16 +92,18 @@ def tile_picked_ymmr_soft_p_kernel(
             for u in range(2)
         ]
 
-        def cast(copy, a, u):
+        def cast(copy, a, u, lo, hi):
             copy(
-                w_bf[u][:, :, :, 2 * a : 2 * a + 2].rearrange("p t m j -> p m t j"),
-                w_raw[a][:].rearrange("p j (m t) -> p m t j", t=PACK)[:, :, 2 * u : 2 * u + 2, :],
+                w_bf[u][:, :, lo:hi, 2 * a : 2 * a + 2].rearrange("p t m j -> p m t j"),
+                w_raw[a][:].rearrange("p j (m t) -> p m t j", t=PACK)[:, lo:hi, 2 * u : 2 * u + 2, :],
             )
 
-        cast(nc.vector.tensor_copy, 0, 1)
-        cast(nc.scalar.copy, 0, 0)
-        cast(nc.scalar.copy, 1, 0)
-        cast(nc.scalar.copy, 1, 1)
+        cast(nc.vector.tensor_copy, 0, 1, 0, P)
+        cast(nc.scalar.copy, 0, 0, 0, P)
+        cast(nc.scalar.copy, 1, 0, 0, P - 4)
+        cast(nc.vector.tensor_copy, 1, 1, 0, 32)
+        cast(nc.scalar.copy, 1, 0, P - 4, P)
+        cast(nc.scalar.copy, 1, 1, 32, P)
 
         xg_first = keep.tile([P, P], U32, name="xg_first", align_bytes=64)
         xg_rest = reuse.tile([P, S - P], U32, name="xg_rest", align_bytes=64, offset=8192)

@@ -75,8 +75,8 @@ def tile_picked_ymmr_soft_p_kernel(
         nc.sync.dma_start(out=second_raw[:, :body], in_=second[:, :body])
         for j in range(4):
             nc.sync.dma_start(out=xs[j:P:32, :].bitcast(I32), in_=x_scales[0, j:16:4, :].bitcast(I32))
-        nc.sync.dma_start(out=second_raw[:, body:], in_=second[:, body:])
         load_words(nc, xw, x_words)
+        nc.sync.dma_start(out=second_raw[:, body:], in_=second[:, body:])
         load_words(nc, ew, e_words)
 
         picked = reuse.tile([P, U + V], U8, name="picked", align_bytes=256, offset=17408)
@@ -102,8 +102,9 @@ def tile_picked_ymmr_soft_p_kernel(
         cast(nc.scalar.copy, 0, 0, 0, P)
         cast(nc.scalar.copy, 1, 0, 0, P - 4)
         cast(nc.vector.tensor_copy, 1, 1, 0, 32)
+        cast(nc.scalar.copy, 1, 1, 32, P - 4)
         cast(nc.scalar.copy, 1, 0, P - 4, P)
-        cast(nc.scalar.copy, 1, 1, 32, P)
+        cast(nc.scalar.copy, 1, 1, P - 4, P)
 
         xg_first = keep.tile([P, P], U32, name="xg_first", align_bytes=64)
         xg_rest = reuse.tile([P, S - P], U32, name="xg_rest", align_bytes=64, offset=8192)
@@ -169,23 +170,35 @@ def tile_picked_ymmr_soft_p_kernel(
 
         def product(bank, i, words, scales):
             nc.tensor.matmul_mx(
-                out=bank[:],
+                out=bank,
                 lhsT=h_q[i][:].bitcast(FP8X4),
                 lhsT_scale=h_s[i][:],
-                rhs=words[:].bitcast(FP8X4),
+                rhs=words.bitcast(FP8X4),
                 rhs_scale=scales,
                 start=True,
                 stop=True,
             )
 
-        eg_w = keep.tile([P, U], U32, name="eg_w", align_bytes=64)
+        eg_w = [
+            keep.tile([P, U // 2], U32, name="eg_a", align_bytes=64),
+            reuse.tile([P, U // 2], U32, name="eg_b", align_bytes=64, offset=17920),
+        ]
         dg_w = keep.tile([P, V], U32, name="dg_w", align_bytes=64)
+
+        def pick_e(c):
+            nc.vector.tensor_copy(eg_w[c][:], ew[:].bitcast(U32).indirect(shown_t[:, 16 * c : 16 * (c + 1)]))
+
+        def pick_d():
+            nc.vector.tensor_copy(dg_w[:], dw[:].bitcast(U32).indirect(user_t[:]))
+
+        pick_e(0)
         quantise(0)
-        nc.vector.tensor_copy(eg_w[:], ew[:].bitcast(U32).indirect(shown_t[:]))
+        pick_e(1)
         quantise(1)
-        nc.vector.tensor_copy(dg_w[:], dw[:].bitcast(U32).indirect(user_t[:]))
+        pick_d()
         quantise(2)
         quantise(3)
+
 
         def pieces(i):
             return [(0, V // 2), (V // 2, V)]
@@ -194,16 +207,29 @@ def tile_picked_ymmr_soft_p_kernel(
         low = reuse.tile([P, TILES, V], F32, name="low", align_bytes=64, offset=1024)
 
         def seen(i):
-            z_ps = psum.tile([P, U], F32, name="z_ps", tag="bank%d" % (4 + i))
-            product(z_ps, i, eg_w, plane[:, :U])
             sig.append(keep.tile([P, D, V], F32, name="sig%d" % i))
-            pairs = z_ps[:].rearrange("p (v d) -> p d v", d=D)
-            for lo, hi in pieces(i):
-                nc.scalar.activation(sig[i][:, :, lo:hi], pairs[:, :, lo:hi], ACT.Sigmoid, scale=-2.0)
+            if i == 0:
+                halves = [psum.tile([P, U // 2], F32, name="z_%d" % c, tag="bank%d" % (4 + c))[:] for c in range(2)]
+            else:
+                z_ps = psum.tile([P, U], F32, name="z_ps", tag="bank%d" % ((5 + i) % 8))
+                halves = [z_ps[:, c * (U // 2) : (c + 1) * (U // 2)] for c in range(2)]
+            for c in range(2):
+                product(halves[c], i, eg_w[c][:], plane[:, c * (U // 2) : (c + 1) * (U // 2)])
+            for c in range(2):
+                nc.scalar.activation(
+                    sig[i][:, :, c * (V // 2) : (c + 1) * (V // 2)],
+                    halves[c].rearrange("p (v d) -> p d v", d=D),
+                    ACT.Sigmoid,
+                    scale=-2.0,
+                )
+
+        y_pair = []
 
         def score(i):
-            y_ps.append(psum.tile([P, V], F32, name="y_ps", tag="bank%d" % i))
-            product(y_ps[i], i, dg_w, plane[:, U:])
+            if i % 2 == 0:
+                y_pair.append(psum.tile([P, 2, V], F32, name="y_ps", tag="bank%d" % (1 + i // 2)))
+            y_ps.append(y_pair[i // 2][:, i % 2, :])
+            product(y_ps[i], i, dg_w[:], plane[:, U:])
 
         for pair in ((0, 1), (2, 3)):
             for i in pair:

@@ -114,7 +114,7 @@ def tile_picked_ymmr_soft_p_kernel(
 
         xg_s = keep.tile([P, S], U8, name="xg_s", align_bytes=64)
         w_q = keep.tile([P, H], U32, name="w_q", align_bytes=64)
-        w_s = reuse.tile([P, H], U8, name="w_s", align_bytes=64, offset=16384)
+        w_s = keep.tile([P, H], U8, name="w_s", align_bytes=64)
 
         def quantise_w(u):
             wc = slice(u * HALF, (u + 1) * HALF)
@@ -132,9 +132,12 @@ def tile_picked_ymmr_soft_p_kernel(
         quantise_w(0)
         quantise_w(1)
         pick_x(P, 2 * P)
-        pick_x(2 * P, S)
+        pick_x(2 * P, 3 * P)
+        pick_x(3 * P, S)
 
         h_q, h_s, h_bf = [], [], []
+        first_bf = keep.tile([P, P, PACK], BF16, name="first_bf", align_bytes=64)
+        late_bf = reuse.tile([P, 3, P, PACK], BF16, name="late_bf", align_bytes=64, offset=14400)
         for i in range(TILES):
             cols = slice(i * P, (i + 1) * P)
             h_ps = psum.tile([P, PACK, P], F32, name="h_ps", tag="bank%d" % i)
@@ -149,21 +152,21 @@ def tile_picked_ymmr_soft_p_kernel(
                     start=True,
                     stop=True,
                 )
-            stage = keep.tile([P, P, PACK], BF16, name="h_bf%d" % i, align_bytes=64)
-            nc.scalar.copy(stage[:], h_ps[:].rearrange("p t n -> p n t"))
+            stage = late_bf[:, i - 1] if i >= 1 else first_bf[:]
+            nc.scalar.copy(stage, h_ps[:].rearrange("p t n -> p n t"))
             h_bf.append(stage)
 
         def quantise(i):
             codes = reuse.tile(
-                [P, P], U32, name="h_codes%d" % i, align_bytes=64, offset=512 * (i - 2) if i >= 2 else 12288 + 512 * i
+                [P, P], U32, name="h_codes%d" % i, align_bytes=64, offset=12288 + 512 * i
             )
             planes = reuse.tile(
-                [P, P], U8, name="h_planes%d" % i, align_bytes=64, offset=17408 + P * i
+                [P, P], U8, name="h_planes%d" % i, align_bytes=64, offset=17472 + P * i
             )
             nc.vector.quantize_mx(
                 out=codes[:].bitcast(FP8X4),
                 scales=planes[:],
-                in_=h_bf[i][:].rearrange("p n t -> p (n t)"),
+                in_=h_bf[i].rearrange("p n t -> p (n t)"),
             )
             h_q.append(codes)
             h_s.append(planes)
@@ -181,7 +184,7 @@ def tile_picked_ymmr_soft_p_kernel(
 
         eg_w = [
             keep.tile([P, U // 2], U32, name="eg_a", align_bytes=64),
-            reuse.tile([P, U // 2], U32, name="eg_b", align_bytes=64, offset=17920),
+            reuse.tile([P, U // 2], U32, name="eg_b", align_bytes=64, offset=18112),
         ]
         dg_w = keep.tile([P, V], U32, name="dg_w", align_bytes=64)
 

@@ -98,11 +98,13 @@ def tile_picked_ymmr_soft_p_kernel(
                 w_raw[a][:].rearrange("p j (m t) -> p m t j", t=PACK)[:, lo:hi, 2 * u : 2 * u + 2, :],
             )
 
-        cast(nc.vector.tensor_copy, 0, 1, 0, P)
+        def round_on_gpsimd(dst, src):
+            nc.gpsimd.tensor_scalar(dst, src, 1.0, 0.0, ALU.mult, ALU.add)
+
+        cast(round_on_gpsimd, 0, 1, 0, P)
         cast(nc.scalar.copy, 0, 0, 0, P)
         cast(nc.scalar.copy, 1, 0, 0, P - 4)
-        cast(nc.vector.tensor_copy, 1, 1, 0, 32)
-        cast(nc.scalar.copy, 1, 1, 32, P - 4)
+        cast(round_on_gpsimd, 1, 1, 0, P - 4)
         cast(nc.scalar.copy, 1, 0, P - 4, P)
         cast(nc.scalar.copy, 1, 1, P - 4, P)
 
@@ -204,7 +206,7 @@ def tile_picked_ymmr_soft_p_kernel(
 
 
         def pieces(i):
-            return [(0, V // 2), (V // 2, V)]
+            return [(0, V // 2), (V // 2, V)] if i < TILES - 1 else [(0, V // 2), (V // 2, 3 * V // 4), (3 * V // 4, V)]
 
         sig, y_ps = [], []
         low = reuse.tile([P, TILES, V], F32, name="low", align_bytes=64, offset=1024)
@@ -218,12 +220,11 @@ def tile_picked_ymmr_soft_p_kernel(
                 halves = [z_ps[:, c * (U // 2) : (c + 1) * (U // 2)] for c in range(2)]
             for c in range(2):
                 product(halves[c], i, eg_w[c][:], plane[:, c * (U // 2) : (c + 1) * (U // 2)])
-            for c in range(2):
+            for lo, hi in pieces(i):
+                c = lo // (V // 2)
+                pairs = halves[c].rearrange("p (v d) -> p d v", d=D)
                 nc.scalar.activation(
-                    sig[i][:, :, c * (V // 2) : (c + 1) * (V // 2)],
-                    halves[c].rearrange("p (v d) -> p d v", d=D),
-                    ACT.Sigmoid,
-                    scale=-2.0,
+                    sig[i][:, :, lo:hi], pairs[:, :, lo - c * (V // 2) : hi - c * (V // 2)], ACT.Sigmoid, scale=-2.0
                 )
 
         y_pair = []
@@ -248,7 +249,8 @@ def tile_picked_ymmr_soft_p_kernel(
         def finish(i, lo, hi):
             nc.vector.tensor_tensor(res[i][:, lo:hi], y_ps[i][:, lo:hi], low[:, i, lo:hi], ALU.mult)
             if i == TILES - 1:
-                nc.sync.dma_start(out=out[i * P : (i + 1) * P, lo:hi], in_=res[i][:, lo:hi])
+                if hi % (V // 2) == 0:
+                    nc.sync.dma_start(out=out[i * P : (i + 1) * P, hi - V // 2 : hi], in_=res[i][:, hi - V // 2 : hi])
             elif hi == V:
                 nc.sync.dma_start(out=out[i * P : (i + 1) * P, :], in_=res[i][:])
 

@@ -213,13 +213,17 @@ def tile_picked_ymmr_soft_p_kernel(
 
         def seen(i):
             sig.append(keep.tile([P, D, V], F32, name="sig%d" % i))
-            if i == 0:
-                halves = [psum.tile([P, U // 2], F32, name="z_%d" % c, tag="bank%d" % (4 + c))[:] for c in range(2)]
-            else:
-                z_ps = psum.tile([P, U], F32, name="z_ps", tag="bank%d" % ((5 + i) % 8))
+            if i == 1:
+                z_ps = psum.tile([P, U], F32, name="z_ps", tag="bank6")
                 halves = [z_ps[:, c * (U // 2) : (c + 1) * (U // 2)] for c in range(2)]
+            else:
+                banks = {0: (4, 5), 2: (7, 3), 3: (0, 4)}[i]
+                halves = [psum.tile([P, U // 2], F32, name="z_%d" % c, tag="bank%d" % banks[c])[:] for c in range(2)]
             for c in range(2):
                 product(halves[c], i, eg_w[c][:], plane[:, c * (U // 2) : (c + 1) * (U // 2)])
+            if i == 1:
+                nc.scalar.activation(sig[i][:], z_ps[:].rearrange("p (v d) -> p d v", d=D), ACT.Sigmoid, scale=-2.0)
+                return
             for lo, hi in pieces(i):
                 c = lo // (V // 2)
                 pairs = halves[c].rearrange("p (v d) -> p d v", d=D)

@@ -50,28 +50,22 @@ def tile_picked_ymmr_soft_p_kernel(
 
         nc.gpsimd.memset(xs[:].bitcast(I32), 0)
         nc.gpsimd.memset(warm[:], 0.0)
-        nc.vector.memset(ds[:96, :].bitcast(I32), 0)
-        nc.vector.memset(es[:96, :].bitcast(I32), 0)
+        nc.vector.memset(ds[:112, :].bitcast(I32), 0)
+        nc.vector.memset(es[:112, :].bitcast(I32), 0)
         nc.vector.memset(plane[:].bitcast(I32), 0)
 
         nc.sync.dma_start(user_t[:], user)
-        nc.scalar.dma_start(
-            out=ds[96:, :].bitcast(I32),
-            in_=d_scales[0].bitcast(I32).unsqueeze(1).broadcast_to([16, 2, G // 4]),
-        )
+        nc.scalar.dma_start(out=ds[112:, :].bitcast(I32), in_=d_scales[0].bitcast(I32))
         nc.sync.dma_start(shown_t[:], shown)
-        nc.scalar.dma_start(
-            out=es[96:, :].bitcast(I32),
-            in_=e_scales[0].bitcast(I32).unsqueeze(1).broadcast_to([16, 2, W // 4]),
-        )
+        nc.scalar.dma_start(out=es[112:, :].bitcast(I32), in_=e_scales[0].bitcast(I32))
         nc.scalar.activation(warm_out[:], warm[:], ACT.Sigmoid, scale=-2.0)
         w_rows = w1.rearrange("(p j) c -> p j c", j=PACK)
         w_raw = [keep.tile([P, 2, H], F32, name="w_raw%d" % a, align_bytes=256) for a in range(2)]
         second = w_rows[:, 2:4, :].rearrange("p j c -> p (j c)")
         second_raw = w_raw[1][:].rearrange("p j c -> p (j c)")
         body = 2 * H - 16
-        nc.sync.dma_start(offs_t[:], offs)
         nc.sync.dma_start(out=w_raw[0][:], in_=w_rows[:, 0:2, :])
+        nc.sync.dma_start(offs_t[:], offs)
         nc.sync.dma_start(out=second_raw[:, :body], in_=second[:, :body])
         for j in range(4):
             nc.sync.dma_start(out=xs[j:P:32, :].bitcast(I32), in_=x_scales[0, j:16:4, :].bitcast(I32))
@@ -83,7 +77,7 @@ def tile_picked_ymmr_soft_p_kernel(
         nc.vector.tensor_copy(picked[:, U:], ds[:].indirect(user_t[:]))
         nc.vector.tensor_copy(picked[:, :U], es[:].indirect(shown_t[:]))
         for j in range(4):
-            nc.sync.dma_start(out=plane[j:P:32, :].bitcast(I32), in_=picked[96 + 2 * j : P : 8, :].bitcast(I32))
+            nc.sync.dma_start(out=plane[j:P:32, :].bitcast(I32), in_=picked[112 + j : P : 4, :].bitcast(I32))
         dw = reuse.tile([P, G], I32, name="dw", align_bytes=256, offset=0)
         load_words(nc, dw, d_words)
 

from contextlib import ExitStack

import concourse.mybir as mybir

K, T, S, H, D, V, W, U, G = 512, 1024, 512, 512, 2, 256, 2048, 512, 1024
FLOPS = 2 * K * H * S + 2 * H * S * V + 2 * H * S * U

F32 = mybir.dt.float32
BF16 = mybir.dt.bfloat16
I32 = mybir.dt.int32
U32 = mybir.dt.uint32
U16 = mybir.dt.uint16
U8 = mybir.dt.uint8
FP8X4 = mybir.dt.float8_e4m3fn_x4
ALU = mybir.AluOpType
ACT = mybir.ActivationFunctionType

P = 128
PACK = 4
TILES = S // P
HALF = H // 2


def load_words(nc, tile, words):
    nc.sync.dma_start(out=tile[:], in_=words[0].rearrange("p n t -> p (n t)").bitcast(I32))


def tile_picked_ymmr_soft_p_kernel(
    tc, x_words, x_scales, w1, e_words, e_scales, d_words, d_scales, offs, user, shown, out
):
    nc = tc.nc
    with ExitStack() as ctx:
        lists = ctx.enter_context(tc.tile_pool(name="lists", bufs=1))
        keep = ctx.enter_context(tc.tile_pool(name="keep", bufs=1))
        reuse = ctx.enter_context(tc.tile_pool(name="reuse", bufs=1))
        psum = ctx.enter_context(tc.psum_pool(name="psum", bufs=1))

        offs_t = lists.tile([P, S // 16], U16, name="offs_t")
        shown_t = lists.tile([P, U // 16], U16, name="shown_t")
        user_t = lists.tile([P, V // 16], U16, name="user_t")

        xw = keep.tile([P, T], I32, name="xw", align_bytes=256)
        ew = keep.tile([P, W], I32, name="ew", align_bytes=256)
        xs = keep.tile([P, T], U8, name="xs", align_bytes=256)
        es = reuse.tile([P, W], U8, name="es", align_bytes=256, offset=0)
        ds = keep.tile([P, G], U8, name="ds", align_bytes=256)
        plane = keep.tile([P, U + V], U8, name="plane", align_bytes=256)
        warm = keep.tile([P, 8], F32, name="warm")
        warm_out = keep.tile([P, 8], F32, name="warm_out")

        nc.gpsimd.memset(xs[:].bitcast(I32), 0)
        nc.gpsimd.memset(warm[:], 0.0)
        nc.vector.memset(ds[:112, :].bitcast(I32), 0)
        nc.vector.memset(es[:112, :].bitcast(I32), 0)
        nc.vector.memset(plane[:].bitcast(I32), 0)

        nc.sync.dma_start(user_t[:], user)
        nc.scalar.dma_start(out=ds[112:, :].bitcast(I32), in_=d_scales[0].bitcast(I32))
        nc.sync.dma_start(shown_t[:], shown)
        nc.scalar.dma_start(out=es[112:, :].bitcast(I32), in_=e_scales[0].bitcast(I32))
        nc.scalar.activation(warm_out[:], warm[:], ACT.Sigmoid, scale=-2.0)
        w_rows = w1.rearrange("(p j) c -> p j c", j=PACK)
        w_raw = [keep.tile([P, 2, H], F32, name="w_raw%d" % a, align_bytes=256) for a in range(2)]
        second = w_rows[:, 2:4, :].rearrange("p j c -> p (j c)")
        second_raw = w_raw[1][:].rearrange("p j c -> p (j c)")
        body = 2 * H - 16
        nc.sync.dma_start(out=w_raw[0][:], in_=w_rows[:, 0:2, :])
        nc.sync.dma_start(offs_t[:], offs)
        nc.sync.dma_start(out=second_raw[:, :body], in_=second[:, :body])
        for j in range(4):
            nc.sync.dma_start(out=xs[j:P:32, :].bitcast(I32), in_=x_scales[0, j:16:4, :].bitcast(I32))
        load_words(nc, xw, x_words)
        nc.sync.dma_start(out=second_raw[:, body:], in_=second[:, body:])
        load_words(nc, ew, e_words)

        picked = reuse.tile([P, U + V], U8, name="picked", align_bytes=256, offset=17408)
        nc.vector.tensor_copy(picked[:, U:], ds[:].indirect(user_t[:]))
        nc.vector.tensor_copy(picked[:, :U], es[:].indirect(shown_t[:]))
        for j in range(4):
            nc.sync.dma_start(out=plane[j:P:32, :].bitcast(I32), in_=picked[112 + j : P : 4, :].bitcast(I32))
        dw = reuse.tile([P, G], I32, name="dw", align_bytes=256, offset=0)
        load_words(nc, dw, d_words)

        w_bf = [
            reuse.tile([P, 2, P, PACK], BF16, name="w_bf%d" % u, align_bytes=64, offset=8192 + 2048 * u)
            for u in range(2)
        ]

        def cast(copy, a, u, lo, hi):
            copy(
                w_bf[u][:, :, lo:hi, 2 * a : 2 * a + 2].rearrange("p t m j -> p m t j"),
                w_raw[a][:].rearrange("p j (m t) -> p m t j", t=PACK)[:, lo:hi, 2 * u : 2 * u + 2, :],
            )

        def round_on_gpsimd(dst, src):
            nc.gpsimd.tensor_scalar(dst, src, 1.0, 0.0, ALU.mult, ALU.add)

        cast(round_on_gpsimd, 0, 1, 0, P)
        cast(nc.scalar.copy, 0, 0, 0, P)
        cast(nc.scalar.copy, 1, 0, 0, P - 4)
        cast(round_on_gpsimd, 1, 1, 0, P - 4)
        cast(nc.scalar.copy, 1, 0, P - 4, P)
        cast(nc.scalar.copy, 1, 1, P - 4, P)

        xg_first = keep.tile([P, P], U32, name="xg_first", align_bytes=64)
        xg_rest = reuse.tile([P, S - P], U32, name="xg_rest", align_bytes=64, offset=8192)

        def xg_w(lo, hi):
            return xg_first[:, lo:hi] if hi <= P else xg_rest[:, lo - P : hi - P]

        xg_s = keep.tile([P, S], U8, name="xg_s", align_bytes=64)
        w_q = keep.tile([P, H], U32, name="w_q", align_bytes=64)
        w_s = keep.tile([P, H], U8, name="w_s", align_bytes=64)

        def quantise_w(u):
            wc = slice(u * HALF, (u + 1) * HALF)
            nc.vector.quantize_mx(
                out=w_q[:, wc].bitcast(FP8X4),
                scales=w_s[:, wc],
                in_=w_bf[u][:].rearrange("p t m j -> p (t m j)"),
            )

        def pick_x(lo, hi):
            nc.vector.tensor_copy(xg_w(lo, hi), xw[:].bitcast(U32).indirect(offs_t[:, lo // 16 : hi // 16]))

        nc.vector.tensor_copy(xg_s[:], xs[:].indirect(offs_t[:]))
        pick_x(0, P)
        quantise_w(0)
        quantise_w(1)
        pick_x(P, 2 * P)
        pick_x(2 * P, 3 * P)
        pick_x(3 * P, S)

        h_q, h_s, h_bf = [], [], []
        first_bf = keep.tile([P, P, PACK], BF16, name="first_bf", align_bytes=64)
        late_bf = reuse.tile([P, 3, P, PACK], BF16, name="late_bf", align_bytes=64, offset=14400)
        for i in range(TILES):
            cols = slice(i * P, (i + 1) * P)
            h_ps = psum.tile([P, PACK, P], F32, name="h_ps", tag="bank%d" % i)
            for t in range(PACK):
                wc = slice(t * P, (t + 1) * P)
                nc.tensor.matmul_mx(
                    out=h_ps[:, t, :],
                    lhsT=w_q[:, wc].bitcast(FP8X4),
                    lhsT_scale=w_s[:, wc],
                    rhs=xg_w(i * P, (i + 1) * P).bitcast(FP8X4),
                    rhs_scale=xg_s[:, cols],
                    start=True,
                    stop=True,
                )
            stage = late_bf[:, i - 1] if i >= 1 else first_bf[:]
            nc.scalar.copy(stage, h_ps[:].rearrange("p t n -> p n t"))
            h_bf.append(stage)

        def quantise(i):
            codes = reuse.tile(
                [P, P], U32, name="h_codes%d" % i, align_bytes=64, offset=12288 + 512 * i
            )
            planes = reuse.tile(
                [P, P], U8, name="h_planes%d" % i, align_bytes=64, offset=17472 + P * i
            )
            nc.vector.quantize_mx(
                out=codes[:].bitcast(FP8X4),
                scales=planes[:],
                in_=h_bf[i].rearrange("p n t -> p (n t)"),
            )
            h_q.append(codes)
            h_s.append(planes)

        def product(bank, i, words, scales):
            nc.tensor.matmul_mx(
                out=bank,
                lhsT=h_q[i][:].bitcast(FP8X4),
                lhsT_scale=h_s[i][:],
                rhs=words.bitcast(FP8X4),
                rhs_scale=scales,
                start=True,
                stop=True,
            )

        eg_w = [
            keep.tile([P, U // 2], U32, name="eg_a", align_bytes=64),
            reuse.tile([P, U // 2], U32, name="eg_b", align_bytes=64, offset=18112),
        ]
        dg_w = keep.tile([P, V], U32, name="dg_w", align_bytes=64)

        def pick_e(c):
            nc.vector.tensor_copy(eg_w[c][:], ew[:].bitcast(U32).indirect(shown_t[:, 16 * c : 16 * (c + 1)]))

        def pick_d():
            nc.vector.tensor_copy(dg_w[:], dw[:].bitcast(U32).indirect(user_t[:]))

        pick_e(0)
        quantise(0)
        pick_e(1)
        quantise(1)
        pick_d()
        quantise(2)
        quantise(3)


        def pieces(i):
            return [(0, V // 2), (V // 2, V)] if i < TILES - 1 else [(0, V // 2), (V // 2, 3 * V // 4), (3 * V // 4, V)]

        sig, y_ps = [], []
        low = reuse.tile([P, TILES, V], F32, name="low", align_bytes=64, offset=1024)

        def seen(i):
            sig.append(keep.tile([P, D, V], F32, name="sig%d" % i))
            if i == 1:
                z_ps = psum.tile([P, U], F32, name="z_ps", tag="bank6")
                halves = [z_ps[:, c * (U // 2) : (c + 1) * (U // 2)] for c in range(2)]
            else:
                banks = {0: (4, 5), 2: (7, 3), 3: (0, 4)}[i]
                halves = [psum.tile([P, U // 2], F32, name="z_%d" % c, tag="bank%d" % banks[c])[:] for c in range(2)]
            for c in range(2):
                product(halves[c], i, eg_w[c][:], plane[:, c * (U // 2) : (c + 1) * (U // 2)])
            if i == 1:
                nc.scalar.activation(sig[i][:], z_ps[:].rearrange("p (v d) -> p d v", d=D), ACT.Sigmoid, scale=-2.0)
                return
            for lo, hi in pieces(i):
                c = lo // (V // 2)
                pairs = halves[c].rearrange("p (v d) -> p d v", d=D)
                nc.scalar.activation(
                    sig[i][:, :, lo:hi], pairs[:, :, lo - c * (V // 2) : hi - c * (V // 2)], ACT.Sigmoid, scale=-2.0
                )

        y_pair = []

        def score(i):
            if i % 2 == 0:
                y_pair.append(psum.tile([P, 2, V], F32, name="y_ps", tag="bank%d" % (1 + i // 2)))
            y_ps.append(y_pair[i // 2][:, i % 2, :])
            product(y_ps[i], i, dg_w[:], plane[:, U:])

        for pair in ((0, 1), (2, 3)):
            for i in pair:
                seen(i)
            for i in pair:
                score(i)

        res = [keep.tile([P, V], F32, name="res%d" % i, align_bytes=256) for i in range(TILES)]

        def lesser(i, lo, hi):
            nc.vector.tensor_tensor(low[:, i, lo:hi], sig[i][:, 0, lo:hi], sig[i][:, 1, lo:hi], ALU.min)

        def finish(i, lo, hi):
            nc.vector.tensor_tensor(res[i][:, lo:hi], y_ps[i][:, lo:hi], low[:, i, lo:hi], ALU.mult)
            if i == TILES - 1:
                if hi % (V // 2) == 0:
                    nc.sync.dma_start(out=out[i * P : (i + 1) * P, hi - V // 2 : hi], in_=res[i][:, hi - V // 2 : hi])
            elif hi == V:
                nc.sync.dma_start(out=out[i * P : (i + 1) * P, :], in_=res[i][:])

        steps = [(i, lo, hi) for i in range(TILES) for lo, hi in pieces(i)]
        for n in range(len(steps) + 1):
            if n < len(steps):
                lesser(*steps[n])
            if n >= 1:
                finish(*steps[n - 1])
